import numpy as np
import ml_dtypes


def mxq(x, axis, fmt="e4m3"):
    dtype, down = {"e4m3": (ml_dtypes.float8_e4m3fn, 7), "e5m2": (ml_dtypes.float8_e5m2, 14)}[fmt]
    v = np.moveaxis(np.asarray(x, np.float32).astype(ml_dtypes.bfloat16).astype(np.float64), axis, -1)
    blocks = v.reshape(v.shape[:-1] + (-1, 32))
    amax = np.abs(blocks).max(-1, keepdims=True)
    byte = np.maximum(np.where(amax > 0, np.frexp(amax)[1] - 1 + 127, 0) - down, 1)
    scale = np.exp2(byte - 127.0)
    codes = (blocks / scale).astype(np.float32).astype(dtype).astype(np.float64)
    return np.moveaxis((codes * scale).reshape(v.shape), -1, axis)


WIDE = False


def mx_kscale(k):
    if not WIDE:
        return np.ones(k)
    levels = np.array([10, -10, 5, -5, 0])
    if k % 512:
        return np.exp2(np.random.permutation(np.resize(levels, k // 32))).repeat(32)
    a = np.empty((k // 512, 16))
    for p in range(k // 512):
        a[p, :8] = np.random.permutation(np.resize(levels, 8))
        for g in range(8):
            far = levels[np.abs(levels - a[p, g]) >= 10]
            a[p, g + 8] = far[np.random.randint(len(far))]
    return np.exp2(a.ravel()).repeat(32)


def f64(x):
    return np.asarray(x).astype(np.float64)


def striped(idx):
    return np.tile(idx.reshape(-1, 16).T, (8, 1)).astype(np.uint16)


def unstriped(offs):
    return offs[:16].T.reshape(-1).astype(np.int64)


E2M1 = np.array([0.0, 0.5, 1.0, 1.5, 2.0, 3.0, 4.0, 6.0, -0.0, -0.5, -1.0, -1.5, -2.0, -3.0, -4.0, -6.0])


def pack_weight(w, fmt):
    k, n = w.shape
    w = f64(np.asarray(w, np.float32).astype(ml_dtypes.bfloat16)).reshape(k // 32, 32, n)
    amax = np.abs(w).max(1)
    if fmt == "e4m3":
        byte = np.frexp(amax)[1] - 1 + 127 - 7
    else:
        mant, ex = np.frexp(amax / 6.0)
        byte = np.where(mant > 0.5, ex, ex - 1) + 127
    byte = np.clip(np.where(amax > 0, byte, 1), 1, 254)
    scaled = (w * np.exp2(127.0 - byte)[:, None, :]).reshape(k, n).astype(np.float32)
    by_word = np.ascontiguousarray(scaled.reshape(k // 512, 128, 4, n).transpose(0, 1, 3, 2))
    if fmt == "e4m3":
        words = by_word.astype(ml_dtypes.float8_e4m3fn).view(np.uint8)
    else:
        c = by_word.astype(ml_dtypes.float4_e2m1fn).view(np.uint8) & 0xF
        words = (c[..., 0::2] | (c[..., 1::2] << 4)).reshape(k // 512, 128, 2 * n)
    return np.ascontiguousarray(words), np.ascontiguousarray(byte.astype(np.uint8).reshape(k // 512, 16, n))


def unpack_weight(words, scales, fmt):
    g, _, n = scales.shape
    words = np.ascontiguousarray(words).reshape(g, 128, n, -1)
    if fmt == "e4m3":
        vals = words.view(ml_dtypes.float8_e4m3fn).astype(np.float64)
    else:
        nib = np.empty((g, 128, n, 4), np.uint8)
        nib[..., 0::2] = words & 0xF
        nib[..., 1::2] = words >> 4
        vals = E2M1[nib]
    vals = vals * np.repeat(np.exp2(scales.astype(np.float64) - 127.0), 8, axis=1)[..., None]
    return vals.transpose(0, 1, 3, 2).reshape(g * 512, n)


def gelu(v):
    return 0.5 * v * (1.0 + np.tanh(np.sqrt(2.0 / np.pi) * (v + 0.044715 * v**3)))


K, H, N, T, S = 1024, 1536, 512, 2048, 1024

def setup_inputs():
    n = np.random.standard_normal
    s = mx_kscale(K)[:, None]
    u = mx_kscale(H)[:, None]
    tab_words, tab_scales = pack_weight(n((K, T)) * s, "e4m3")
    ws_words, ws_scales = pack_weight(0.8 * n((K, N)) / np.sqrt(K) / s, "e2m1")
    return {
        "tab_words": tab_words,
        "tab_scales": tab_scales,
        "offs": striped(np.random.permutation(T)[:S]),
        "w1": (n((K, H)) / np.sqrt(K) / s * u.T).astype(np.float32),
        "b1": (0.5 * n(H) * u[:, 0]).astype(np.float32),
        "w2": (1.3 * n((H, N)) / np.sqrt(H) / u).astype(np.float32),
        "ws_words": ws_words,
        "ws_scales": ws_scales,
        "b2": (0.5 * n(N)).astype(np.float32),
    }

def reference(tab_words, tab_scales, offs, w1, b1, w2, ws_words, ws_scales, b2):
    v = unpack_weight(tab_words, tab_scales, "e4m3")[:, unstriped(offs)]
    ws = unpack_weight(ws_words, ws_scales, "e2m1")
    w1q = mxq(f64(w1), 0, "e4m3")
    w2q = mxq(f64(w2), 0, "e4m3")
    h = np.maximum((w1q.T @ v) + f64(b1)[:, None], 0.0)
    hq = mxq(h, 0, "e4m3")
    y = w2q.T @ hq + ws.T @ v
    return y + f64(b2)[:, None]

@@ -1,0 +1,322 @@
+from contextlib import ExitStack
+
+import concourse.mybir as mybir
+
+K, H, N, T, S = 1024, 1536, 512, 2048, 1024
+FLOPS = 2 * S * (K * H + H * N + K * N)
+
+F32 = mybir.dt.float32
+BF16 = mybir.dt.bfloat16
+I32 = mybir.dt.int32
+U32 = mybir.dt.uint32
+U16 = mybir.dt.uint16
+U8 = mybir.dt.uint8
+FP8X4 = mybir.dt.float8_e4m3fn_x4
+FP4X4 = mybir.dt.float4_e2m1fn_x4
+ACT = mybir.ActivationFunctionType
+ALU = mybir.AluOpType
+
+P = 128
+PACK = 4
+K_PASS = P * PACK
+HALF = 512
+KP = K // K_PASS
+HP = H // K_PASS
+NT = N // P
+
+LOADS = ["offs", "b1", "ts", ("w1", 0, 0), ("tw", 0), ("w1", 0, 1), ("tw", 1), ("w1", 1, 0), ("w1", 1, 1), "b2", ("w1", 2, 0), "wss", ("w1", 2, 1), "ws", ("w2", 0), ("w2", 1), ("w2", 2)]
+PLAN = [
+    ("gs", 0, 0, 1024),
+    ("gs", 1, 0, 1024),
+    ("c", ("w1", 0, 0), "SS"),
+    ("gw", 0, 0, 512),
+    ("gw", 0, 512, 1024),
+    ("c", ("w1", 0, 1), "VS"),
+    ("q", ("w1", 0, 0)),
+    ("q", ("w1", 0, 1)),
+    ("gw", 1, 0, 512),
+    ("gw", 1, 512, 1024),
+    ("L", 0, 0, 0, "S"),
+    ("L", 0, 0, 1, "S"),
+    ("L", 0, 0, 2, "S"),
+    ("L", 0, 0, 3, "S"),
+    ("c", ("w1", 1, 0), "VV"),
+    ("q", ("w1", 1, 0)),
+    ("L", 0, 1, 0, "V"),
+    ("L", 0, 1, 1, "S"),
+    ("c", ("w1", 1, 1), "VS"),
+    ("L", 0, 1, 2, "S"),
+    ("L", 0, 1, 3, "S"),
+    ("c", ("h", 0, 0), "VV"),
+    ("q", ("w1", 1, 1)),
+    ("c", ("w1", 2, 0), "SV"),
+    ("L", 1, 0, 0, "V"),
+    ("q", ("w1", 2, 0)),
+    ("L", 1, 0, 1, "S"),
+    ("L", 1, 0, 2, "S"),
+    ("L", 1, 0, 3, "S"),
+    ("q", ("h", 0, 0)),
+    ("c", ("w1", 2, 1), "VV"),
+    ("L", 1, 1, 0, "S"),
+    ("L", 1, 1, 1, "S"),
+    ("L", 1, 1, 2, "S"),
+    ("L", 1, 1, 3, "S"),
+    ("c", ("h", 0, 1), "VV"),
+    ("q", ("w1", 2, 1)),
+    ("skip", 0, (0,)),
+    ("skip", 0, (1,)),
+    ("c", ("h", 1, 0), "SS"),
+    ("c", ("w2", 0), "VV"),
+    ("L", 2, 0, 0, "S"),
+    ("L", 2, 0, 1, "S"),
+    ("L", 2, 0, 2, "S"),
+    ("L", 2, 0, 3, "S"),
+    ("q", ("h", 0, 1)),
+    ("c", ("w2", 1), "VV"),
+    ("skip", 0, (2,)),
+    ("L", 2, 1, 0, "S"),
+    ("L", 2, 1, 1, "S"),
+    ("L", 2, 1, 2, "S"),
+    ("L", 2, 1, 3, "V"),
+    ("q", ("w2", 0)),
+    ("c", ("w2", 2), "VV"),
+    ("skip", 0, (3,)),
+    ("skip", 1, (0,)),
+    ("skip", 1, (1,)),
+    ("y", 0, 0, (0, 1,)),
+    ("y", 0, 0, (2, 3,)),
+    ("skip", 1, (2,)),
+    ("skip", 1, (3,)),
+    ("y", 0, 1, (0, 1,)),
+    ("y", 0, 1, (2, 3,)),
+    ("c", ("h", 2, 0), "SV"),
+    ("q", ("w2", 2)),
+    ("q", ("h", 2, 0)),
+    ("q", ("h", 1, 0)),
+    ("q", ("w2", 1)),
+    ("c", ("h", 2, 1), "SS"),
+    ("y", 2, 0, (0, 1,)),
+    ("y", 2, 0, (2, 3,)),
+    ("y", 1, 0, (0, 1,)),
+    ("y", 1, 0, (2, 3,)),
+    ("c", ("h", 1, 1), "VV"),
+    ("q", ("h", 2, 1)),
+    ("q", ("h", 1, 1)),
+    ("o", 0, (0,), "S"),
+    ("o", 0, (1,), "S"),
+    ("o", 0, (2,), "S"),
+    ("o", 0, (3,), "V"),
+    ("y", 2, 1, (0, 1,)),
+    ("y", 1, 1, (0, 1,)),
+    ("y", 2, 1, (2, 3,)),
+    ("y", 1, 1, (2, 3,)),
+    ("o", 1, (0,), "V"),
+    ("o", 1, (1,), "S"),
+    ("o", 1, (2,), "V"),
+    ("o", 1, (3,), "S"),
+]
+
+
+def tile_list_paged_skip_adapter_kernel(
+    tc, tab_words, tab_scales, offs, w1, b1, w2, ws_words, ws_scales, b2, out
+):
+    nc = tc.nc
+    with ExitStack() as ctx:
+        keep = ctx.enter_context(tc.tile_pool(name="keep", bufs=1))
+        stage = ctx.enter_context(tc.tile_pool(name="stage", bufs=3))
+        psum = ctx.enter_context(tc.psum_pool(name="psum", bufs=1))
+
+        offsets = keep.tile([P, S // 16], U16, name="offsets")
+        tw = [keep.tile([P, T], I32, name=f"tw{a}", align_bytes=64) for a in range(KP)]
+        ts = keep.tile([P, KP, T // 4], I32, name="ts", align_bytes=64)
+        vw = [keep.tile([P, S], U32, name=f"vw{a}", align_bytes=64) for a in range(KP)]
+        vs = [keep.tile([P, S], U8, name=f"vs{a}", align_bytes=64) for a in range(KP)]
+        wsw = keep.tile([P, KP, 2 * N], U8, name="wsw", align_bytes=64)
+        wss = keep.tile([P, KP, N], U8, name="wss", align_bytes=64)
+        b1t = keep.tile([P, HP, PACK], F32, name="b1t")
+        b2t = keep.tile([P, NT], F32, name="b2t")
+        raw = {}
+        codes = {}
+        planes = {}
+        for key in [("w1", b, a) for b in range(HP) for a in range(KP)] + [("w2", b) for b in range(HP)]:
+            nm = "".join(str(x) for x in key)
+            raw[key] = keep.tile([P, PACK, K_PASS], F32, name="raw" + nm, align_bytes=64)
+            codes[key] = keep.tile([P, K_PASS], U32, name="codes" + nm, align_bytes=64)
+            planes[key] = keep.tile([P, K_PASS], U8, name="plane" + nm, align_bytes=64)
+        for key in [("h", b, s) for b in range(HP) for s in range(2)]:
+            nm = "".join(str(x) for x in key)
+            codes[key] = keep.tile([P, HALF], U32, name="codes" + nm, align_bytes=64)
+            planes[key] = keep.tile([P, HALF], U8, name="plane" + nm, align_bytes=64)
+
+        banks = [psum.tile([P, HALF], F32, name=f"bank{n}") for n in range(8)]
+        free_banks = list(range(8))
+        ybank = {}
+
+        def take_bank():
+            n = free_banks[0]
+            free_banks.remove(n)
+            return n
+
+        nc.vector.memset(ts[:, 0, :], 0)
+        nc.gpsimd.memset(ts[:, 1, :], 0)
+        nc.vector.memset(wss[:].bitcast(I32), 0)
+
+        def load(key):
+            if key == "offs":
+                nc.sync.dma_start(offsets[:], offs)
+            elif key == "ts":
+                for q in range(4):
+                    nc.sync.dma_start(
+                        ts[32 * q : 32 * q + 4, :, :],
+                        tab_scales[:, 4 * q : 4 * q + 4, :].rearrange("a r c -> r a c").bitcast(I32),
+                    )
+            elif key == "ws":
+                nc.sync.dma_start(wsw[:].bitcast(I32), ws_words.rearrange("a p c -> p a c").bitcast(I32))
+            elif key == "wss":
+                for q in range(4):
+                    nc.sync.dma_start(
+                        wss[32 * q : 32 * q + 4, :, :].bitcast(I32),
+                        ws_scales[:, 4 * q : 4 * q + 4, :].rearrange("a r c -> r a c").bitcast(I32),
+                    )
+            elif key == "b1":
+                nc.sync.dma_start(b1t[:], b1.rearrange("(b p t) -> p b t", p=P, t=PACK))
+            elif key == "b2":
+                with nc.allow_non_contiguous_dma(reason="one bias value for each partition"):
+                    nc.sync.dma_start(b2t[:], b2.rearrange("(u p) -> p u", p=P))
+            elif key[0] == "tw":
+                a = key[1]
+                nc.sync.dma_start(tw[a][:], tab_words[a].rearrange("p t i -> p (t i)").bitcast(I32))
+            elif key[0] == "w1":
+                b, a = key[1:]
+                rows = w1[a * K_PASS : (a + 1) * K_PASS, b * K_PASS : (b + 1) * K_PASS]
+                nc.sync.dma_start(raw[key][:], rows.rearrange("(p j) c -> p j c", j=PACK))
+            else:
+                b = key[1]
+                rows = w2[b * K_PASS : (b + 1) * K_PASS, :]
+                nc.sync.dma_start(raw[key][:], rows.rearrange("(p j) c -> p j c", j=PACK))
+
+        for key in LOADS:
+            load(key)
+
+        def copy(engine, dst, src):
+            if engine == "V":
+                nc.vector.tensor_copy(out=dst, in_=src)
+            else:
+                nc.scalar.copy(out=dst, in_=src)
+
+        grouped = {}
+        flat = {}
+        ytile = {}
+        passes = {}
+
+        def y_pass(s, u):
+            n = passes.get((s, u), 0)
+            passes[(s, u)] = n + 1
+            if n == 0:
+                ybank[(s, u)] = take_bank()
+                ytile[(s, u)] = banks[ybank[(s, u)]]
+            return ytile[(s, u)][:], n == 0, n == KP + HP - 1
+
+        def cast(key, engines):
+            g = stage.tile([P, K_PASS * PACK], BF16, name="grouped", align_bytes=64, bufs=8)
+            grouped[key] = g
+            parts = len(engines)
+            if key[0] == "w1":
+                dst = g[:].rearrange("p (t m j) -> p m j t", t=PACK, j=PACK)
+                src = raw[key][:].rearrange("p j (m t) -> p m j t", t=PACK)
+            else:
+                source = raw[key] if key[0] == "w2" else flat[key]
+                dst = g[:].rearrange("p (m i j) -> p m j i", i=PACK, j=PACK)
+                src = source[:].rearrange("p j (m i) -> p m j i", i=PACK)
+            width = P // parts
+            for n, engine in enumerate(engines):
+                copy(engine, dst[:, n * width : (n + 1) * width], src[:, n * width : (n + 1) * width])
+
+        def quantise(key):
+            nc.vector.quantize_mx(out=codes[key][:].bitcast(FP8X4), scales=planes[key][:], in_=grouped[key][:])
+
+        def gather(kind, a, first, last):
+            picks = offsets[:, first // 16 : last // 16]
+            if kind == "gw":
+                nc.vector.tensor_copy(vw[a][:, first:last], tw[a][:].bitcast(U32).indirect(picks))
+            else:
+                nc.vector.tensor_copy(vs[a][:, first:last], ts[:, a, :].bitcast(U8).indirect(picks))
+
+        def hidden(b, s, t, engine):
+            cols = slice(s * HALF, (s + 1) * HALF)
+            if ("h", b, s) not in flat:
+                flat[("h", b, s)] = stage.tile([P, PACK, HALF], BF16, name="flat", align_bytes=64, bufs=4)
+            f = flat[("h", b, s)]
+            bank = take_bank()
+            acc = banks[bank]
+            for a in range(KP):
+                key = ("w1", b, a)
+                nc.tensor.matmul_mx(
+                    acc[:],
+                    lhsT=codes[key][:, t * P : (t + 1) * P].bitcast(FP8X4),
+                    lhsT_scale=planes[key][:, t * P : (t + 1) * P],
+                    rhs=vw[a][:, cols].bitcast(FP8X4),
+                    rhs_scale=vs[a][:, cols],
+                    start=(a == 0),
+                    stop=(a == KP - 1),
+                )
+            if engine == "S":
+                nc.scalar.activation(f[:, t, :], acc[:], ACT.Relu, bias=b1t[:, b, t : t + 1])
+            else:
+                nc.vector.tensor_scalar(f[:, t, :], acc[:], b1t[:, b, t : t + 1], 0.0, op0=ALU.add, op1=ALU.max)
+            free_banks.append(bank)
+
+        def skip(s, tiles):
+            cols = slice(s * HALF, (s + 1) * HALF)
+            for u in tiles:
+                for a in range(KP):
+                    acc, first, last = y_pass(s, u)
+                    nc.tensor.matmul_mx(
+                        acc,
+                        lhsT=wsw[:, a, 2 * u * P : 2 * (u + 1) * P].bitcast(FP4X4),
+                        lhsT_scale=wss[:, a, u * P : (u + 1) * P],
+                        rhs=vw[a][:, cols].bitcast(FP8X4),
+                        rhs_scale=vs[a][:, cols],
+                        start=first,
+                        stop=last,
+                    )
+
+        def second(b, s, tiles):
+            for u in tiles:
+                acc, first, last = y_pass(s, u)
+                nc.tensor.matmul_mx(
+                    acc,
+                    lhsT=codes[("w2", b)][:, u * P : (u + 1) * P].bitcast(FP8X4),
+                    lhsT_scale=planes[("w2", b)][:, u * P : (u + 1) * P],
+                    rhs=codes[("h", b, s)][:].bitcast(FP8X4),
+                    rhs_scale=planes[("h", b, s)][:],
+                    start=first,
+                    stop=last,
+                )
+
+        def finish(s, tiles, engines):
+            for u, engine in zip(tiles, engines):
+                res = keep.tile([P, HALF], F32, name=f"res{s}{u}")
+                if engine == "S":
+                    nc.scalar.activation(res[:], ytile[(s, u)][:], ACT.Identity, bias=b2t[:, u : u + 1])
+                else:
+                    nc.vector.tensor_scalar(res[:], ytile[(s, u)][:], b2t[:, u : u + 1], None, op0=ALU.add)
+                free_banks.append(ybank[(s, u)])
+                nc.sync.dma_start(out[u * P : (u + 1) * P, s * HALF : (s + 1) * HALF], res[:])
+
+        for step in PLAN:
+            kind = step[0]
+            if kind in ("gw", "gs"):
+                gather(*step)
+            elif kind == "c":
+                cast(step[1], step[2])
+            elif kind == "q":
+                quantise(step[1])
+            elif kind == "L":
+                hidden(*step[1:])
+            elif kind == "skip":
+                skip(*step[1:])
+            elif kind == "y":
+                second(*step[1:])
+            else:
+                finish(*step[1:])

@@ -24,96 +24,106 @@ KP = K // K_PASS
 HP = H // K_PASS
 NT = N // P
 
-LOADS = ["offs", "b1", "ts", ("w1", 0, 0), ("tw", 0), ("w1", 0, 1), ("tw", 1), ("w1", 1, 0), ("w1", 1, 1), "b2", ("w1", 2, 0), "wss", ("w1", 2, 1), "ws", ("w2", 0), ("w2", 1), ("w2", 2)]
+LOADS = ["offs", "b1", "ts", ("w1", 0, 0, 0, 512), ("tw", 0), ("w1", 0, 1, 0, 256), ("tw", 1), ("w1", 0, 1, 256, 512), ("w1", 1, 0, 0, 512), ("w1", 1, 1, 0, 512), ("w1", 2, 0, 0, 512), ("w1", 2, 1, 0, 512), "wss", "ws", ("w2", 1), ("w2", 0), ("w2", 2), "b2"]
 PLAN = [
     ("gs", 0, 0, 1024),
     ("gs", 1, 0, 1024),
-    ("c", ("w1", 0, 0), "SS"),
-    ("gw", 0, 0, 512),
-    ("gw", 0, 512, 1024),
-    ("c", ("w1", 0, 1), "VS"),
+    ("c", ("w1", 0, 0), "S"),
     ("q", ("w1", 0, 0)),
+    ("gw", 0, 0, 1024),
+    ("gw", 1, 0, 1024),
+    ("c", ("w1", 0, 1), "SS"),
     ("q", ("w1", 0, 1)),
-    ("gw", 1, 0, 512),
-    ("gw", 1, 512, 1024),
-    ("L", 0, 0, 0, "S"),
-    ("L", 0, 0, 1, "S"),
-    ("L", 0, 0, 2, "S"),
+    ("c", ("w1", 1, 0), "SV"),
+    ("L", 0, 0, 1, "V"),
     ("L", 0, 0, 3, "S"),
-    ("c", ("w1", 1, 0), "VV"),
     ("q", ("w1", 1, 0)),
-    ("L", 0, 1, 0, "V"),
+    ("L", 0, 0, 2, "S"),
+    ("c", ("w1", 1, 1), "V"),
+    ("L", 0, 0, 0, "S"),
     ("L", 0, 1, 1, "S"),
-    ("c", ("w1", 1, 1), "VS"),
-    ("L", 0, 1, 2, "S"),
-    ("L", 0, 1, 3, "S"),
-    ("c", ("h", 0, 0), "VV"),
+    ("L", 0, 1, 0, "S"),
     ("q", ("w1", 1, 1)),
+    ("L", 0, 1, 3, "S"),
     ("c", ("w1", 2, 0), "SV"),
-    ("L", 1, 0, 0, "V"),
+    ("c", ("h", 0, 0), "VV"),
+    ("L", 1, 0, 0, "S"),
+    ("L", 0, 1, 2, "V"),
+    ("L", 1, 1, 0, "S"),
     ("q", ("w1", 2, 0)),
-    ("L", 1, 0, 1, "S"),
-    ("L", 1, 0, 2, "S"),
     ("L", 1, 0, 3, "S"),
     ("q", ("h", 0, 0)),
-    ("c", ("w1", 2, 1), "VV"),
-    ("L", 1, 1, 0, "S"),
     ("L", 1, 1, 1, "S"),
+    ("c", ("w1", 2, 1), "V"),
+    ("L", 1, 0, 2, "S"),
+    ("skip", 0, (3,)),
+    ("L", 1, 0, 1, "S"),
+    ("skip", 1, (3,)),
+    ("c", ("h", 0, 1), "V"),
     ("L", 1, 1, 2, "S"),
     ("L", 1, 1, 3, "S"),
-    ("c", ("h", 0, 1), "VV"),
     ("q", ("w1", 2, 1)),
-    ("skip", 0, (0,)),
-    ("skip", 0, (1,)),
-    ("c", ("h", 1, 0), "SS"),
-    ("c", ("w2", 0), "VV"),
-    ("L", 2, 0, 0, "S"),
-    ("L", 2, 0, 1, "S"),
-    ("L", 2, 0, 2, "S"),
-    ("L", 2, 0, 3, "S"),
+    ("c", ("h", 1, 0), "V"),
+    ("skip", 1, (0,)),
     ("q", ("h", 0, 1)),
-    ("c", ("w2", 1), "VV"),
-    ("skip", 0, (2,)),
-    ("L", 2, 1, 0, "S"),
+    ("L", 2, 0, 2, "S"),
+    ("q", ("h", 1, 0)),
+    ("L", 2, 0, 3, "S"),
+    ("c", ("w2", 0), "V"),
     ("L", 2, 1, 1, "S"),
     ("L", 2, 1, 2, "S"),
-    ("L", 2, 1, 3, "V"),
+    ("c", ("w2", 1), "VS"),
+    ("skip", 0, (2,)),
+    ("L", 2, 1, 0, "S"),
     ("q", ("w2", 0)),
-    ("c", ("w2", 2), "VV"),
-    ("skip", 0, (3,)),
-    ("skip", 1, (0,)),
-    ("skip", 1, (1,)),
-    ("y", 0, 0, (0, 1,)),
-    ("y", 0, 0, (2, 3,)),
-    ("skip", 1, (2,)),
-    ("skip", 1, (3,)),
-    ("y", 0, 1, (0, 1,)),
-    ("y", 0, 1, (2, 3,)),
-    ("c", ("h", 2, 0), "SV"),
-    ("q", ("w2", 2)),
-    ("q", ("h", 2, 0)),
-    ("q", ("h", 1, 0)),
+    ("L", 2, 0, 0, "S"),
+    ("skip", 0, (1,)),
     ("q", ("w2", 1)),
-    ("c", ("h", 2, 1), "SS"),
-    ("y", 2, 0, (0, 1,)),
-    ("y", 2, 0, (2, 3,)),
-    ("y", 1, 0, (0, 1,)),
-    ("y", 1, 0, (2, 3,)),
-    ("c", ("h", 1, 1), "VV"),
-    ("q", ("h", 2, 1)),
-    ("q", ("h", 1, 1)),
-    ("o", 0, (0,), "S"),
-    ("o", 0, (1,), "S"),
+    ("L", 2, 0, 1, "S"),
+    ("y", 0, 1, (3,)),
+    ("y", 0, 0, (2,)),
+    ("c", ("w2", 2), "V"),
+    ("L", 2, 1, 3, "S"),
+    ("y", 1, 0, (3,)),
+    ("y", 0, 0, (3,)),
+    ("y", 1, 0, (2,)),
+    ("c", ("h", 2, 0), "SV"),
+    ("skip", 0, (0,)),
+    ("skip", 1, (2,)),
+    ("q", ("w2", 2)),
+    ("y", 1, 0, (0,)),
+    ("y", 0, 0, (0,)),
+    ("q", ("h", 2, 0)),
+    ("skip", 1, (1,)),
+    ("c", ("h", 1, 1), "VS"),
+    ("y", 0, 1, (0,)),
+    ("y", 2, 0, (2,)),
+    ("c", ("h", 2, 1), "VS"),
+    ("y", 2, 0, (3,)),
+    ("y", 2, 0, (0,)),
     ("o", 0, (2,), "S"),
-    ("o", 0, (3,), "V"),
-    ("y", 2, 1, (0, 1,)),
-    ("y", 1, 1, (0, 1,)),
-    ("y", 2, 1, (2, 3,)),
-    ("y", 1, 1, (2, 3,)),
-    ("o", 1, (0,), "V"),
-    ("o", 1, (1,), "S"),
-    ("o", 1, (2,), "V"),
+    ("y", 2, 0, (1,)),
+    ("q", ("h", 1, 1)),
+    ("y", 0, 0, (1,)),
+    ("o", 0, (3,), "S"),
+    ("y", 1, 0, (1,)),
+    ("q", ("h", 2, 1)),
+    ("y", 1, 1, (3,)),
+    ("o", 0, (0,), "S"),
+    ("y", 1, 1, (2,)),
+    ("y", 2, 1, (3,)),
+    ("o", 0, (1,), "S"),
+    ("y", 2, 1, (0,)),
+    ("y", 1, 1, (0,)),
     ("o", 1, (3,), "S"),
+    ("y", 2, 1, (2,)),
+    ("y", 0, 1, (2,)),
+    ("o", 1, (0,), "V"),
+    ("y", 2, 1, (1,)),
+    ("y", 1, 1, (1,)),
+    ("o", 1, (2,), "S"),
+    ("y", 0, 1, (1,)),
+    ("o", 1, (1,), "S"),
 ]
 
 
@@ -187,9 +197,9 @@ def tile_list_paged_skip_adapter_kernel(
                 a = key[1]
                 nc.sync.dma_start(tw[a][:], tab_words[a].rearrange("p t i -> p (t i)").bitcast(I32))
             elif key[0] == "w1":
-                b, a = key[1:]
-                rows = w1[a * K_PASS : (a + 1) * K_PASS, b * K_PASS : (b + 1) * K_PASS]
-                nc.sync.dma_start(raw[key][:], rows.rearrange("(p j) c -> p j c", j=PACK))
+                b, a, first, last = key[1:]
+                rows = w1[a * K_PASS : (a + 1) * K_PASS, b * K_PASS + first : b * K_PASS + last]
+                nc.sync.dma_start(raw[key[:3]][:, :, first:last], rows.rearrange("(p j) c -> p j c", j=PACK))
             else:
                 b = key[1]
                 rows = w2[b * K_PASS : (b + 1) * K_PASS, :]
@@ -204,6 +214,8 @@ def tile_list_paged_skip_adapter_kernel(
             else:
                 nc.scalar.copy(out=dst, in_=src)
 
+        ring = [keep.tile([P, K_PASS * PACK], BF16, name=f"ring{n}", align_bytes=64) for n in range(4)]
+        free_slots = list(range(4))
         grouped = {}
         flat = {}
         ytile = {}
@@ -218,8 +230,10 @@ def tile_list_paged_skip_adapter_kernel(
             return ytile[(s, u)][:], n == 0, n == KP + HP - 1
 
         def cast(key, engines):
-            g = stage.tile([P, K_PASS * PACK], BF16, name="grouped", align_bytes=64, bufs=8)
-            grouped[key] = g
+            slot = free_slots[0]
+            free_slots.remove(slot)
+            grouped[key] = slot
+            g = ring[slot]
             parts = len(engines)
             if key[0] == "w1":
                 dst = g[:].rearrange("p (t m j) -> p m j t", t=PACK, j=PACK)
@@ -233,7 +247,8 @@ def tile_list_paged_skip_adapter_kernel(
                 copy(engine, dst[:, n * width : (n + 1) * width], src[:, n * width : (n + 1) * width])
 
         def quantise(key):
-            nc.vector.quantize_mx(out=codes[key][:].bitcast(FP8X4), scales=planes[key][:], in_=grouped[key][:])
+            nc.vector.quantize_mx(out=codes[key][:].bitcast(FP8X4), scales=planes[key][:], in_=ring[grouped[key]][:])
+            free_slots.append(grouped[key])
 
         def gather(kind, a, first, last):
             picks = offsets[:, first // 16 : last // 16]

@@ -1,6 +1,7 @@
 from contextlib import ExitStack
 
 import concourse.mybir as mybir
+from concourse.masks import make_identity
 
 K, H, N, T, S = 1024, 1536, 512, 2048, 1024
 FLOPS = 2 * S * (K * H + H * N + K * N)
@@ -20,111 +21,13 @@ P = 128
 PACK = 4
 K_PASS = P * PACK
 HALF = 512
+HALVES = S // HALF
 KP = K // K_PASS
 HP = H // K_PASS
 NT = N // P
-
-LOADS = ["offs", "b1", "ts", ("w1", 0, 0, 0, 512), ("tw", 0), ("w1", 0, 1, 0, 256), ("tw", 1), ("w1", 0, 1, 256, 512), ("w1", 1, 0, 0, 512), ("w1", 1, 1, 0, 512), ("w1", 2, 0, 0, 512), ("w1", 2, 1, 0, 512), "wss", "ws", ("w2", 1), ("w2", 0), ("w2", 2), "b2"]
-PLAN = [
-    ("gs", 0, 0, 1024),
-    ("gs", 1, 0, 1024),
-    ("c", ("w1", 0, 0), "S"),
-    ("q", ("w1", 0, 0)),
-    ("gw", 0, 0, 1024),
-    ("gw", 1, 0, 1024),
-    ("c", ("w1", 0, 1), "SS"),
-    ("q", ("w1", 0, 1)),
-    ("c", ("w1", 1, 0), "SV"),
-    ("L", 0, 0, 1, "V"),
-    ("L", 0, 0, 3, "S"),
-    ("q", ("w1", 1, 0)),
-    ("L", 0, 0, 2, "S"),
-    ("c", ("w1", 1, 1), "V"),
-    ("L", 0, 0, 0, "S"),
-    ("L", 0, 1, 1, "S"),
-    ("L", 0, 1, 0, "S"),
-    ("q", ("w1", 1, 1)),
-    ("L", 0, 1, 3, "S"),
-    ("c", ("w1", 2, 0), "SV"),
-    ("c", ("h", 0, 0), "VV"),
-    ("L", 1, 0, 0, "S"),
-    ("L", 0, 1, 2, "V"),
-    ("L", 1, 1, 0, "S"),
-    ("q", ("w1", 2, 0)),
-    ("L", 1, 0, 3, "S"),
-    ("q", ("h", 0, 0)),
-    ("L", 1, 1, 1, "S"),
-    ("c", ("w1", 2, 1), "V"),
-    ("L", 1, 0, 2, "S"),
-    ("skip", 0, (3,)),
-    ("L", 1, 0, 1, "S"),
-    ("skip", 1, (3,)),
-    ("c", ("h", 0, 1), "V"),
-    ("L", 1, 1, 2, "S"),
-    ("L", 1, 1, 3, "S"),
-    ("q", ("w1", 2, 1)),
-    ("c", ("h", 1, 0), "V"),
-    ("skip", 1, (0,)),
-    ("q", ("h", 0, 1)),
-    ("L", 2, 0, 2, "S"),
-    ("q", ("h", 1, 0)),
-    ("L", 2, 0, 3, "S"),
-    ("c", ("w2", 0), "V"),
-    ("L", 2, 1, 1, "S"),
-    ("L", 2, 1, 2, "S"),
-    ("c", ("w2", 1), "VS"),
-    ("skip", 0, (2,)),
-    ("L", 2, 1, 0, "S"),
-    ("q", ("w2", 0)),
-    ("L", 2, 0, 0, "S"),
-    ("skip", 0, (1,)),
-    ("q", ("w2", 1)),
-    ("L", 2, 0, 1, "S"),
-    ("y", 0, 1, (3,)),
-    ("y", 0, 0, (2,)),
-    ("c", ("w2", 2), "V"),
-    ("L", 2, 1, 3, "S"),
-    ("y", 1, 0, (3,)),
-    ("y", 0, 0, (3,)),
-    ("y", 1, 0, (2,)),
-    ("c", ("h", 2, 0), "SV"),
-    ("skip", 0, (0,)),
-    ("skip", 1, (2,)),
-    ("q", ("w2", 2)),
-    ("y", 1, 0, (0,)),
-    ("y", 0, 0, (0,)),
-    ("q", ("h", 2, 0)),
-    ("skip", 1, (1,)),
-    ("c", ("h", 1, 1), "VS"),
-    ("y", 0, 1, (0,)),
-    ("y", 2, 0, (2,)),
-    ("c", ("h", 2, 1), "VS"),
-    ("y", 2, 0, (3,)),
-    ("y", 2, 0, (0,)),
-    ("o", 0, (2,), "S"),
-    ("y", 2, 0, (1,)),
-    ("q", ("h", 1, 1)),
-    ("y", 0, 0, (1,)),
-    ("o", 0, (3,), "S"),
-    ("y", 1, 0, (1,)),
-    ("q", ("h", 2, 1)),
-    ("y", 1, 1, (3,)),
-    ("o", 0, (0,), "S"),
-    ("y", 1, 1, (2,)),
-    ("y", 2, 1, (3,)),
-    ("o", 0, (1,), "S"),
-    ("y", 2, 1, (0,)),
-    ("y", 1, 1, (0,)),
-    ("o", 1, (3,), "S"),
-    ("y", 2, 1, (2,)),
-    ("y", 0, 1, (2,)),
-    ("o", 1, (0,), "V"),
-    ("y", 2, 1, (1,)),
-    ("y", 1, 1, (1,)),
-    ("o", 1, (2,), "S"),
-    ("y", 0, 1, (1,)),
-    ("o", 1, (1,), "S"),
-]
+QUADRANTS = 4
+BANKS = 8
+STAGING = 4
 
 
 def tile_list_paged_skip_adapter_kernel(
@@ -133,205 +36,233 @@ def tile_list_paged_skip_adapter_kernel(
     nc = tc.nc
     with ExitStack() as ctx:
         keep = ctx.enter_context(tc.tile_pool(name="keep", bufs=1))
-        stage = ctx.enter_context(tc.tile_pool(name="stage", bufs=3))
         psum = ctx.enter_context(tc.psum_pool(name="psum", bufs=1))
 
         offsets = keep.tile([P, S // 16], U16, name="offsets")
-        tw = [keep.tile([P, T], I32, name=f"tw{a}", align_bytes=64) for a in range(KP)]
-        ts = keep.tile([P, KP, T // 4], I32, name="ts", align_bytes=64)
-        vw = [keep.tile([P, S], U32, name=f"vw{a}", align_bytes=64) for a in range(KP)]
-        vs = [keep.tile([P, S], U8, name=f"vs{a}", align_bytes=64) for a in range(KP)]
-        wsw = keep.tile([P, KP, 2 * N], U8, name="wsw", align_bytes=64)
-        wss = keep.tile([P, KP, N], U8, name="wss", align_bytes=64)
-        b1t = keep.tile([P, HP, PACK], F32, name="b1t")
-        b2t = keep.tile([P, NT], F32, name="b2t")
-        raw = {}
-        codes = {}
-        planes = {}
-        for key in [("w1", b, a) for b in range(HP) for a in range(KP)] + [("w2", b) for b in range(HP)]:
-            nm = "".join(str(x) for x in key)
-            raw[key] = keep.tile([P, PACK, K_PASS], F32, name="raw" + nm, align_bytes=64)
-            codes[key] = keep.tile([P, K_PASS], U32, name="codes" + nm, align_bytes=64)
-            planes[key] = keep.tile([P, K_PASS], U8, name="plane" + nm, align_bytes=64)
-        for key in [("h", b, s) for b in range(HP) for s in range(2)]:
-            nm = "".join(str(x) for x in key)
-            codes[key] = keep.tile([P, HALF], U32, name="codes" + nm, align_bytes=64)
-            planes[key] = keep.tile([P, HALF], U8, name="plane" + nm, align_bytes=64)
+        table = [keep.tile([P, T], I32, name=f"table{a}", align_bytes=64) for a in range(KP)]
+        table_scales = keep.tile([P, T // 4], I32, name="table_scales", align_bytes=64)
+        v_words = [keep.tile([P, S], U32, name=f"v_words{a}", align_bytes=64) for a in range(KP)]
+        v_scales = keep.tile([P, S], U8, name="v_scales", align_bytes=64)
+        v_scales_low = keep.tile([P, S // 4], I32, name="v_scales_low", align_bytes=64)
+        skip_words = keep.tile([P, KP, 2 * N], U8, name="skip_words", align_bytes=64)
+        skip_scales = keep.tile([P, KP, N], U8, name="skip_scales", align_bytes=64)
+        bias_rows = keep.tile([P, K_PASS], F32, name="bias_rows")
+        identity = keep.tile([P, P], F32, name="identity")
+        b1_cols = keep.tile([P, PACK, HP], F32, name="b1_cols")
+        b2_cols = keep.tile([P, NT], F32, name="b2_cols")
+        w1_keys = [("w1", b, a) for b in range(HP) for a in range(KP)]
+        w2_keys = [("w2", b) for b in range(HP)]
+        h_keys = [("h", b, s) for b in range(HP) for s in range(HALVES)]
+        planes, codes, scales = {}, {}, {}
+        for key in w1_keys + w2_keys + h_keys:
+            label = "".join(str(part) for part in key)
+            dtype = BF16 if key[0] == "h" else F32
+            planes[key] = keep.tile([P, PACK, K_PASS], dtype, name="planes_" + label, align_bytes=64)
+            codes[key] = keep.tile([P, K_PASS], U32, name="codes_" + label, align_bytes=64)
+            scales[key] = keep.tile([P, K_PASS], U8, name="scales_" + label, align_bytes=64)
+        staging = [keep.tile([P, K_PASS * PACK], BF16, name=f"staging{n}", align_bytes=64) for n in range(STAGING)]
+        banks = [psum.tile([P, HALF], F32, name=f"bank{n}") for n in range(BANKS)]
 
-        banks = [psum.tile([P, HALF], F32, name=f"bank{n}") for n in range(8)]
-        free_banks = list(range(8))
-        ybank = {}
+        nc.vector.memset(table_scales[:, : T // 8], 0)
+        nc.gpsimd.memset(table_scales[:, T // 8 :], 0)
+        nc.gpsimd.memset(bias_rows[:], 0.0)
+        make_identity(nc, identity[:])
+        nc.gpsimd.memset(skip_scales[:].bitcast(I32), 0)
+        nc.gpsimd.memset(v_scales_low[:], 0)
 
-        def take_bank():
-            n = free_banks[0]
-            free_banks.remove(n)
-            return n
+        def load_table(a, first=0, last=T):
+            words = tab_words[a].rearrange("p t i -> p (t i)").bitcast(I32)
+            nc.sync.dma_start(table[a][:, first:last], words[:, first:last])
 
-        nc.vector.memset(ts[:, 0, :], 0)
-        nc.gpsimd.memset(ts[:, 1, :], 0)
-        nc.vector.memset(wss[:].bitcast(I32), 0)
+        def load_w1(b, a, first=0, last=K_PASS):
+            rows = w1[a * K_PASS : (a + 1) * K_PASS, b * K_PASS + first : b * K_PASS + last]
+            nc.sync.dma_start(planes[("w1", b, a)][:, :, first:last], rows.rearrange("(p j) c -> p j c", j=PACK))
 
-        def load(key):
-            if key == "offs":
-                nc.sync.dma_start(offsets[:], offs)
-            elif key == "ts":
-                for q in range(4):
-                    nc.sync.dma_start(
-                        ts[32 * q : 32 * q + 4, :, :],
-                        tab_scales[:, 4 * q : 4 * q + 4, :].rearrange("a r c -> r a c").bitcast(I32),
-                    )
-            elif key == "ws":
-                nc.sync.dma_start(wsw[:].bitcast(I32), ws_words.rearrange("a p c -> p a c").bitcast(I32))
-            elif key == "wss":
-                for q in range(4):
-                    nc.sync.dma_start(
-                        wss[32 * q : 32 * q + 4, :, :].bitcast(I32),
-                        ws_scales[:, 4 * q : 4 * q + 4, :].rearrange("a r c -> r a c").bitcast(I32),
-                    )
-            elif key == "b1":
-                nc.sync.dma_start(b1t[:], b1.rearrange("(b p t) -> p b t", p=P, t=PACK))
-            elif key == "b2":
-                with nc.allow_non_contiguous_dma(reason="one bias value for each partition"):
-                    nc.sync.dma_start(b2t[:], b2.rearrange("(u p) -> p u", p=P))
-            elif key[0] == "tw":
-                a = key[1]
-                nc.sync.dma_start(tw[a][:], tab_words[a].rearrange("p t i -> p (t i)").bitcast(I32))
-            elif key[0] == "w1":
-                b, a, first, last = key[1:]
-                rows = w1[a * K_PASS : (a + 1) * K_PASS, b * K_PASS + first : b * K_PASS + last]
-                nc.sync.dma_start(raw[key[:3]][:, :, first:last], rows.rearrange("(p j) c -> p j c", j=PACK))
-            else:
-                b = key[1]
-                rows = w2[b * K_PASS : (b + 1) * K_PASS, :]
-                nc.sync.dma_start(raw[key][:], rows.rearrange("(p j) c -> p j c", j=PACK))
+        def load_w2(b):
+            rows = w2[b * K_PASS : (b + 1) * K_PASS, :]
+            nc.sync.dma_start(planes[("w2", b)][:], rows.rearrange("(p j) c -> p j c", j=PACK))
 
-        for key in LOADS:
-            load(key)
+        def load_skip():
+            for q in range(QUADRANTS):
+                nc.sync.dma_start(
+                    skip_scales[32 * q : 32 * q + 4, :, :].bitcast(I32),
+                    ws_scales[:, 4 * q : 4 * q + 4, :].rearrange("a r c -> r a c").bitcast(I32),
+                )
+            nc.sync.dma_start(skip_words[:].bitcast(I32), ws_words.rearrange("a p c -> p a c").bitcast(I32))
 
-        def copy(engine, dst, src):
-            if engine == "V":
-                nc.vector.tensor_copy(out=dst, in_=src)
-            else:
-                nc.scalar.copy(out=dst, in_=src)
+        nc.sync.dma_start(offsets[:], offs)
+        load_table(0, 0, T // 4)
+        for q in range(QUADRANTS):
+            nc.sync.dma_start(table_scales[32 * q : 32 * q + 8, :], tab_scales[:, 4 * q : 4 * q + 4, :].bitcast(I32))
+        load_table(0, T // 4, T)
+        load_w1(0, 0)
+        nc.sync.dma_start(bias_rows[0:HP, :], b1.rearrange("(b c) -> b c", b=HP))
+        nc.sync.dma_start(bias_rows[HP : HP + 1, :], b2.rearrange("(o c) -> o c", o=1))
+        load_w1(0, 1)
+        load_table(1)
+        for a in range(KP):
+            load_w1(1, a)
 
-        ring = [keep.tile([P, K_PASS * PACK], BF16, name=f"ring{n}", align_bytes=64) for n in range(4)]
-        free_slots = list(range(4))
-        grouped = {}
-        flat = {}
-        ytile = {}
-        passes = {}
+        for t in range(PACK):
+            nc.tensor.transpose(banks[6][:, t * P : (t + 1) * P], bias_rows[:, t::PACK], identity[:])
+        for u in range(NT):
+            nc.tensor.transpose(banks[7][:, u * P : (u + 1) * P], bias_rows[:, u * P : (u + 1) * P], identity[:])
+        nc.scalar.copy(out=b1_cols[:], in_=banks[6][:].rearrange("p (t r) -> p t r", t=PACK)[:, :, 0:HP])
+        nc.scalar.copy(out=b2_cols[:], in_=banks[7][:].rearrange("p (u r) -> p u r", u=NT)[:, :, HP])
 
-        def y_pass(s, u):
-            n = passes.get((s, u), 0)
-            passes[(s, u)] = n + 1
-            if n == 0:
-                ybank[(s, u)] = take_bank()
-                ytile[(s, u)] = banks[ybank[(s, u)]]
-            return ytile[(s, u)][:], n == 0, n == KP + HP - 1
+        staged = {}
 
-        def cast(key, engines):
-            slot = free_slots[0]
-            free_slots.remove(slot)
-            grouped[key] = slot
-            g = ring[slot]
-            parts = len(engines)
+        def interleave(key, engines, slot):
+            tile = staging[slot]
+            staged[key] = tile
             if key[0] == "w1":
-                dst = g[:].rearrange("p (t m j) -> p m j t", t=PACK, j=PACK)
-                src = raw[key][:].rearrange("p j (m t) -> p m j t", t=PACK)
+                dst = tile[:].rearrange("p (t m j) -> p m j t", t=PACK, j=PACK)
             else:
-                source = raw[key] if key[0] == "w2" else flat[key]
-                dst = g[:].rearrange("p (m i j) -> p m j i", i=PACK, j=PACK)
-                src = source[:].rearrange("p j (m i) -> p m j i", i=PACK)
-            width = P // parts
+                dst = tile[:].rearrange("p (m i j) -> p m j i", i=PACK, j=PACK)
+            src = planes[key][:].rearrange("p j (m i) -> p m j i", i=PACK)
             for n, engine in enumerate(engines):
-                copy(engine, dst[:, n * width : (n + 1) * width], src[:, n * width : (n + 1) * width])
+                if key[0] == "w1":
+                    width = PACK // len(engines)
+                    part = (slice(None), slice(None), slice(None), slice(n * width, (n + 1) * width))
+                else:
+                    width = P // len(engines)
+                    part = (slice(None), slice(n * width, (n + 1) * width))
+                if engine == "V":
+                    nc.vector.tensor_copy(out=dst[part], in_=src[part])
+                else:
+                    nc.scalar.copy(out=dst[part], in_=src[part])
 
         def quantise(key):
-            nc.vector.quantize_mx(out=codes[key][:].bitcast(FP8X4), scales=planes[key][:], in_=ring[grouped[key]][:])
-            free_slots.append(grouped[key])
+            nc.vector.quantize_mx(out=codes[key][:].bitcast(FP8X4), scales=scales[key][:], in_=staged[key][:])
 
-        def gather(kind, a, first, last):
-            picks = offsets[:, first // 16 : last // 16]
-            if kind == "gw":
-                nc.vector.tensor_copy(vw[a][:, first:last], tw[a][:].bitcast(U32).indirect(picks))
-            else:
-                nc.vector.tensor_copy(vs[a][:, first:last], ts[:, a, :].bitcast(U8).indirect(picks))
-
-        def hidden(b, s, t, engine):
-            cols = slice(s * HALF, (s + 1) * HALF)
-            if ("h", b, s) not in flat:
-                flat[("h", b, s)] = stage.tile([P, PACK, HALF], BF16, name="flat", align_bytes=64, bufs=4)
-            f = flat[("h", b, s)]
-            bank = take_bank()
-            acc = banks[bank]
-            for a in range(KP):
-                key = ("w1", b, a)
-                nc.tensor.matmul_mx(
-                    acc[:],
-                    lhsT=codes[key][:, t * P : (t + 1) * P].bitcast(FP8X4),
-                    lhsT_scale=planes[key][:, t * P : (t + 1) * P],
-                    rhs=vw[a][:, cols].bitcast(FP8X4),
-                    rhs_scale=vs[a][:, cols],
-                    start=(a == 0),
-                    stop=(a == KP - 1),
+        def prepare_w1(key, slot):
+            tile = staging[slot]
+            dst = tile[:].rearrange("p (t m j) -> p m j t", t=PACK, j=PACK)
+            src = planes[key][:].rearrange("p j (m t) -> p m j t", t=PACK)
+            for pair in range(2):
+                part = slice(2 * pair, 2 * pair + 2)
+                nc.vector.tensor_copy(out=dst[:, :, :, part], in_=src[:, :, :, part])
+            for pair in range(2):
+                part = slice(2 * pair * P, 2 * (pair + 1) * P)
+                nc.vector.quantize_mx(
+                    out=codes[key][:, part].bitcast(FP8X4),
+                    scales=scales[key][:, part],
+                    in_=tile[:, PACK * part.start : PACK * part.stop],
                 )
+
+        def prepare(key, engines, slot):
+            interleave(key, engines, slot)
+            quantise(key)
+
+        def h_bank(b, s, t):
+            return banks[NT * s + t] if b + 1 < HP else banks[NT + t]
+
+        def hidden_pass(b, s, t, a, order):
+            cols = slice(s * HALF, (s + 1) * HALF)
+            key = ("w1", b, a)
+            nc.tensor.matmul_mx(
+                h_bank(b, s, t)[:],
+                lhsT=codes[key][:, t * P : (t + 1) * P].bitcast(FP8X4),
+                lhsT_scale=scales[key][:, t * P : (t + 1) * P],
+                rhs=v_words[a][:, cols].bitcast(FP8X4),
+                rhs_scale=v_scales[4 * a :, cols],
+                start=(a == order[0]),
+                stop=(a == order[-1]),
+            )
+
+        def hidden(b, s):
+            order = list(range(KP))
+            if HALVES * b + s > 2:
+                order = order[::-1]
+            for t in range(PACK):
+                for a in order:
+                    hidden_pass(b, s, t, a, order)
+                nc.scalar.activation(
+                    planes[("h", b, s)][:, t, :], h_bank(b, s, t)[:], ACT.Relu, bias=b1_cols[:, t, b : b + 1]
+                )
+
+        def y_bank(s, u):
+            return banks[NT * s + u]
+
+        def skip_pass(a, s, u):
+            cols = slice(s * HALF, (s + 1) * HALF)
+            low = v_scales[:] if a == 0 else v_scales_low[:].bitcast(U8)
+            nc.tensor.matmul_mx(
+                y_bank(s, u)[:],
+                lhsT=skip_words[:, a, 2 * u * P : 2 * (u + 1) * P].bitcast(FP4X4),
+                lhsT_scale=skip_scales[:, a, u * P : (u + 1) * P],
+                rhs=v_words[a][:, cols].bitcast(FP8X4),
+                rhs_scale=low[:, cols],
+                start=(a == 0),
+                stop=False,
+            )
+
+        def main_pass(b, s, u, last):
+            nc.tensor.matmul_mx(
+                y_bank(s, u)[:],
+                lhsT=codes[("w2", b)][:, u * P : (u + 1) * P].bitcast(FP8X4),
+                lhsT_scale=scales[("w2", b)][:, u * P : (u + 1) * P],
+                rhs=codes[("h", b, s)][:].bitcast(FP8X4),
+                rhs_scale=scales[("h", b, s)][:],
+                start=False,
+                stop=last,
+            )
+
+        def finish(s, u, engine):
+            result = keep.tile([P, HALF], F32, name=f"result{s}{u}")
             if engine == "S":
-                nc.scalar.activation(f[:, t, :], acc[:], ACT.Relu, bias=b1t[:, b, t : t + 1])
+                nc.scalar.activation(result[:], y_bank(s, u)[:], ACT.Identity, bias=b2_cols[:, u : u + 1])
             else:
-                nc.vector.tensor_scalar(f[:, t, :], acc[:], b1t[:, b, t : t + 1], 0.0, op0=ALU.add, op1=ALU.max)
-            free_banks.append(bank)
+                nc.vector.tensor_scalar(result[:], y_bank(s, u)[:], b2_cols[:, u : u + 1], None, op0=ALU.add)
+            nc.sync.dma_start(out[u * P : (u + 1) * P, s * HALF : (s + 1) * HALF], result[:])
 
-        def skip(s, tiles):
-            cols = slice(s * HALF, (s + 1) * HALF)
-            for u in tiles:
-                for a in range(KP):
-                    acc, first, last = y_pass(s, u)
-                    nc.tensor.matmul_mx(
-                        acc,
-                        lhsT=wsw[:, a, 2 * u * P : 2 * (u + 1) * P].bitcast(FP4X4),
-                        lhsT_scale=wss[:, a, u * P : (u + 1) * P],
-                        rhs=vw[a][:, cols].bitcast(FP8X4),
-                        rhs_scale=vs[a][:, cols],
-                        start=first,
-                        stop=last,
-                    )
+        def gather_words(a, first, last):
+            picks = offsets[:, first // 16 : last // 16]
+            nc.vector.tensor_copy(v_words[a][:, first:last], table[a][:].bitcast(U32).indirect(picks))
 
-        def second(b, s, tiles):
-            for u in tiles:
-                acc, first, last = y_pass(s, u)
-                nc.tensor.matmul_mx(
-                    acc,
-                    lhsT=codes[("w2", b)][:, u * P : (u + 1) * P].bitcast(FP8X4),
-                    lhsT_scale=planes[("w2", b)][:, u * P : (u + 1) * P],
-                    rhs=codes[("h", b, s)][:].bitcast(FP8X4),
-                    rhs_scale=planes[("h", b, s)][:],
-                    start=first,
-                    stop=last,
-                )
+        nc.vector.tensor_copy(v_scales[:], table_scales[:].bitcast(U8).indirect(offsets[:]))
+        gather_words(0, 0, S)
+        prepare(("w1", 0, 0), "SV", 0)
+        prepare(("w1", 0, 1), "SV", 1)
+        for s in range(HALVES):
+            gather_words(1, s * HALF, (s + 1) * HALF)
+        load_skip()
+        load_w1(2, 0)
+        for q in range(QUADRANTS):
+            nc.sync.dma_start(v_scales_low[32 * q : 32 * q + 4, :], v_scales[32 * q + 4 : 32 * q + 8, :].bitcast(I32))
+        load_w1(2, 1)
+        for b in range(HP):
+            load_w2(b)
 
-        def finish(s, tiles, engines):
-            for u, engine in zip(tiles, engines):
-                res = keep.tile([P, HALF], F32, name=f"res{s}{u}")
-                if engine == "S":
-                    nc.scalar.activation(res[:], ytile[(s, u)][:], ACT.Identity, bias=b2t[:, u : u + 1])
-                else:
-                    nc.vector.tensor_scalar(res[:], ytile[(s, u)][:], b2t[:, u : u + 1], None, op0=ALU.add)
-                free_banks.append(ybank[(s, u)])
-                nc.sync.dma_start(out[u * P : (u + 1) * P, s * HALF : (s + 1) * HALF], res[:])
+        for b in range(HP - 1):
+            for s in range(HALVES):
+                hidden(b, s)
+            for a in range(KP):
+                prepare_w1(("w1", b + 1, a), a)
+            prepare(("h", b, 0), "V" if b == 0 else "SV", 1)
+        for a in range(KP):
+            for u in range(NT):
+                skip_pass(a, 0, u)
+        for s in range(HALVES):
+            hidden(HP - 1, s)
 
-        for step in PLAN:
-            kind = step[0]
-            if kind in ("gw", "gs"):
-                gather(*step)
-            elif kind == "c":
-                cast(step[1], step[2])
-            elif kind == "q":
-                quantise(step[1])
-            elif kind == "L":
-                hidden(*step[1:])
-            elif kind == "skip":
-                skip(*step[1:])
-            elif kind == "y":
-                second(*step[1:])
-            else:
-                finish(*step[1:])
+        for b in range(HP):
+            if b == HP - 1:
+                prepare(("h", b, 0), "V", 2)
+            prepare(("w2", b), "V", b % 2)
+            for u in range(NT):
+                main_pass(b, 0, u, b == HP - 1)
+        for u in range(NT):
+            finish(0, u, "S")
+        prepare(("h", 2, 1), "S", 3)
+        prepare(("h", 0, 1), "V", 2)
+        prepare(("h", 1, 1), "S", 1)
+        for u in range(NT):
+            for a in range(KP):
+                skip_pass(a, 1, u)
+        for b in (2, 0):
+            for u in range(NT):
+                main_pass(b, 1, u, False)
+        for u in range(NT):
+            main_pass(1, 1, u, True)
+            finish(1, u, "SV"[u % 2])

@@ -63,12 +63,11 @@ def tile_list_paged_skip_adapter_kernel(
         staging = [keep.tile([P, K_PASS * PACK], BF16, name=f"staging{n}", align_bytes=64) for n in range(STAGING)]
         banks = [psum.tile([P, HALF], F32, name=f"bank{n}") for n in range(BANKS)]
 
-        nc.vector.memset(table_scales[:, : T // 8], 0)
-        nc.gpsimd.memset(table_scales[:, T // 8 :], 0)
-        nc.gpsimd.memset(bias_rows[:], 0.0)
+        nc.vector.memset(table_scales[:], 0)
+        nc.vector.memset(bias_rows[:], 0.0)
+        nc.vector.memset(skip_scales[:].bitcast(I32), 0)
+        nc.vector.memset(v_scales_low[:], 0)
         make_identity(nc, identity[:])
-        nc.gpsimd.memset(skip_scales[:].bitcast(I32), 0)
-        nc.gpsimd.memset(v_scales_low[:], 0)
 
         def load_table(a, first=0, last=T):
             words = tab_words[a].rearrange("p t i -> p (t i)").bitcast(I32)
@@ -83,21 +82,20 @@ def tile_list_paged_skip_adapter_kernel(
             nc.sync.dma_start(planes[("w2", b)][:], rows.rearrange("(p j) c -> p j c", j=PACK))
 
         def load_skip():
-            for q in range(QUADRANTS):
-                nc.sync.dma_start(
-                    skip_scales[32 * q : 32 * q + 4, :, :].bitcast(I32),
-                    ws_scales[:, 4 * q : 4 * q + 4, :].rearrange("a r c -> r a c").bitcast(I32),
-                )
             nc.sync.dma_start(skip_words[:].bitcast(I32), ws_words.rearrange("a p c -> p a c").bitcast(I32))
 
         nc.sync.dma_start(offsets[:], offs)
-        load_table(0, 0, T // 4)
         for q in range(QUADRANTS):
-            nc.sync.dma_start(table_scales[32 * q : 32 * q + 8, :], tab_scales[:, 4 * q : 4 * q + 4, :].bitcast(I32))
-        load_table(0, T // 4, T)
+            nc.gpsimd.dma_start(table_scales[32 * q : 32 * q + 8, :], tab_scales[:, 4 * q : 4 * q + 4, :].bitcast(I32))
+        for q in range(QUADRANTS):
+            nc.gpsimd.dma_start(
+                skip_scales[32 * q : 32 * q + 4, :, :].bitcast(I32),
+                ws_scales[:, 4 * q : 4 * q + 4, :].rearrange("a r c -> r a c").bitcast(I32),
+            )
+        load_table(0)
+        nc.sync.dma_start(bias_rows[0 : 4 * HP : 4, :], b1.rearrange("(b c) -> b c", b=HP))
+        nc.sync.dma_start(bias_rows[4 * HP : 4 * HP + 1, :], b2.rearrange("(o c) -> o c", o=1))
         load_w1(0, 0)
-        nc.sync.dma_start(bias_rows[0:HP, :], b1.rearrange("(b c) -> b c", b=HP))
-        nc.sync.dma_start(bias_rows[HP : HP + 1, :], b2.rearrange("(o c) -> o c", o=1))
         load_w1(0, 1)
         load_table(1)
         for a in range(KP):
@@ -107,8 +105,8 @@ def tile_list_paged_skip_adapter_kernel(
             nc.tensor.transpose(banks[6][:, t * P : (t + 1) * P], bias_rows[:, t::PACK], identity[:])
         for u in range(NT):
             nc.tensor.transpose(banks[7][:, u * P : (u + 1) * P], bias_rows[:, u * P : (u + 1) * P], identity[:])
-        nc.scalar.copy(out=b1_cols[:], in_=banks[6][:].rearrange("p (t r) -> p t r", t=PACK)[:, :, 0:HP])
-        nc.scalar.copy(out=b2_cols[:], in_=banks[7][:].rearrange("p (u r) -> p u r", u=NT)[:, :, HP])
+        nc.scalar.copy(out=b1_cols[:], in_=banks[6][:].rearrange("p (t r) -> p t r", t=PACK)[:, :, 0 : 4 * HP : 4])
+        nc.scalar.copy(out=b2_cols[:], in_=banks[7][:].rearrange("p (u r) -> p u r", u=NT)[:, :, 4 * HP])
 
         staged = {}
 
@@ -116,14 +114,15 @@ def tile_list_paged_skip_adapter_kernel(
             tile = staging[slot]
             staged[key] = tile
             if key[0] == "w1":
-                dst = tile[:].rearrange("p (t m j) -> p m j t", t=PACK, j=PACK)
+                dst = tile[:].rearrange("p (t m h j) -> p m j h t", t=PACK, h=2, j=PACK)
+                src = planes[key][:].rearrange("p j (m h t) -> p m j h t", h=2, t=PACK)
             else:
                 dst = tile[:].rearrange("p (m i j) -> p m j i", i=PACK, j=PACK)
-            src = planes[key][:].rearrange("p j (m i) -> p m j i", i=PACK)
+                src = planes[key][:].rearrange("p j (m i) -> p m j i", i=PACK)
             for n, engine in enumerate(engines):
                 if key[0] == "w1":
                     width = PACK // len(engines)
-                    part = (slice(None), slice(None), slice(None), slice(n * width, (n + 1) * width))
+                    part = (slice(None), slice(None), slice(None), slice(None), slice(n * width, (n + 1) * width))
                 else:
                     width = P // len(engines)
                     part = (slice(None), slice(n * width, (n + 1) * width))
@@ -137,11 +136,11 @@ def tile_list_paged_skip_adapter_kernel(
 
         def prepare_w1(key, slot):
             tile = staging[slot]
-            dst = tile[:].rearrange("p (t m j) -> p m j t", t=PACK, j=PACK)
-            src = planes[key][:].rearrange("p j (m t) -> p m j t", t=PACK)
+            dst = tile[:].rearrange("p (t m h j) -> p m j h t", t=PACK, h=2, j=PACK)
+            src = planes[key][:].rearrange("p j (m h t) -> p m j h t", h=2, t=PACK)
             for pair in range(2):
                 part = slice(2 * pair, 2 * pair + 2)
-                nc.vector.tensor_copy(out=dst[:, :, :, part], in_=src[:, :, :, part])
+                nc.vector.tensor_copy(out=dst[:, :, :, :, part], in_=src[:, :, :, :, part])
             for pair in range(2):
                 part = slice(2 * pair * P, 2 * (pair + 1) * P)
                 nc.vector.quantize_mx(
@@ -220,19 +219,20 @@ def tile_list_paged_skip_adapter_kernel(
             picks = offsets[:, first // 16 : last // 16]
             nc.vector.tensor_copy(v_words[a][:, first:last], table[a][:].bitcast(U32).indirect(picks))
 
-        nc.vector.tensor_copy(v_scales[:], table_scales[:].bitcast(U8).indirect(offsets[:]))
         gather_words(0, 0, S)
-        prepare(("w1", 0, 0), "SV", 0)
+        nc.vector.tensor_copy(v_scales[:], table_scales[:].bitcast(U8).indirect(offsets[:]))
+        prepare(("w1", 0, 0), "S", 0)
         prepare(("w1", 0, 1), "SV", 1)
         for s in range(HALVES):
             gather_words(1, s * HALF, (s + 1) * HALF)
         load_skip()
-        load_w1(2, 0)
         for q in range(QUADRANTS):
             nc.sync.dma_start(v_scales_low[32 * q : 32 * q + 4, :], v_scales[32 * q + 4 : 32 * q + 8, :].bitcast(I32))
+        load_w1(2, 0)
         load_w1(2, 1)
-        for b in range(HP):
-            load_w2(b)
+        load_w2(0)
+        load_w2(1)
+        load_w2(2)
 
         for b in range(HP - 1):
             for s in range(HALVES):
@@ -260,9 +260,8 @@ def tile_list_paged_skip_adapter_kernel(
         for u in range(NT):
             for a in range(KP):
                 skip_pass(a, 1, u)
-        for b in (2, 0):
-            for u in range(NT):
-                main_pass(b, 1, u, False)
+            main_pass(2, 1, u, False)
         for u in range(NT):
+            main_pass(0, 1, u, False)
             main_pass(1, 1, u, True)
             finish(1, u, "SV"[u % 2])

@@ -40,10 +40,9 @@ def tile_list_paged_skip_adapter_kernel(
 
         offsets = keep.tile([P, S // 16], U16, name="offsets")
         table = [keep.tile([P, T], I32, name=f"table{a}", align_bytes=64) for a in range(KP)]
-        table_scales = keep.tile([P, T // 4], I32, name="table_scales", align_bytes=64)
+        table_scales = keep.tile([P, KP, T // 4], I32, name="table_scales", align_bytes=64)
         v_words = [keep.tile([P, S], U32, name=f"v_words{a}", align_bytes=64) for a in range(KP)]
-        v_scales = keep.tile([P, S], U8, name="v_scales", align_bytes=64)
-        v_scales_low = keep.tile([P, S // 4], I32, name="v_scales_low", align_bytes=64)
+        v_scales = [keep.tile([P, S], U8, name=f"v_scales{a}", align_bytes=64) for a in range(KP)]
         skip_words = keep.tile([P, KP, 2 * N], U8, name="skip_words", align_bytes=64)
         skip_scales = keep.tile([P, KP, N], U8, name="skip_scales", align_bytes=64)
         bias_rows = keep.tile([P, K_PASS], F32, name="bias_rows")
@@ -63,10 +62,10 @@ def tile_list_paged_skip_adapter_kernel(
         staging = [keep.tile([P, K_PASS * PACK], BF16, name=f"staging{n}", align_bytes=64) for n in range(STAGING)]
         banks = [psum.tile([P, HALF], F32, name=f"bank{n}") for n in range(BANKS)]
 
-        nc.vector.memset(table_scales[:], 0)
-        nc.vector.memset(bias_rows[:], 0.0)
+        nc.vector.memset(table_scales[:, 0, :], 0)
+        nc.gpsimd.memset(table_scales[:, 1, :], 0)
         nc.vector.memset(skip_scales[:].bitcast(I32), 0)
-        nc.vector.memset(v_scales_low[:], 0)
+        nc.vector.memset(bias_rows[:], 0.0)
         make_identity(nc, identity[:])
 
         def load_table(a, first=0, last=T):
@@ -81,18 +80,26 @@ def tile_list_paged_skip_adapter_kernel(
             rows = w2[b * K_PASS : (b + 1) * K_PASS, :]
             nc.sync.dma_start(planes[("w2", b)][:], rows.rearrange("(p j) c -> p j c", j=PACK))
 
+        def load_skip_scales(q):
+            nc.sync.dma_start(
+                skip_scales[32 * q : 32 * q + 4, :, :].bitcast(I32),
+                ws_scales[:, 4 * q : 4 * q + 4, :].rearrange("a r c -> r a c").bitcast(I32),
+            )
+
         def load_skip():
             nc.sync.dma_start(skip_words[:].bitcast(I32), ws_words.rearrange("a p c -> p a c").bitcast(I32))
 
         nc.sync.dma_start(offsets[:], offs)
-        for q in range(QUADRANTS):
-            nc.gpsimd.dma_start(table_scales[32 * q : 32 * q + 8, :], tab_scales[:, 4 * q : 4 * q + 4, :].bitcast(I32))
-        for q in range(QUADRANTS):
-            nc.gpsimd.dma_start(
-                skip_scales[32 * q : 32 * q + 4, :, :].bitcast(I32),
-                ws_scales[:, 4 * q : 4 * q + 4, :].rearrange("a r c -> r a c").bitcast(I32),
+        load_table(0, 0, 3 * T // 8)
+        for q in (0, 2, 1, 3):
+            nc.sync.dma_start(
+                table_scales[32 * q : 32 * q + 4, :, :],
+                tab_scales[:, 4 * q : 4 * q + 4, :].rearrange("a r c -> r a c").bitcast(I32),
             )
-        load_table(0)
+        for q in (0, 2, 1):
+            load_skip_scales(q)
+        load_table(0, 3 * T // 8, T)
+        load_skip_scales(3)
         nc.sync.dma_start(bias_rows[0 : 4 * HP : 4, :], b1.rearrange("(b c) -> b c", b=HP))
         nc.sync.dma_start(bias_rows[4 * HP : 4 * HP + 1, :], b2.rearrange("(o c) -> o c", o=1))
         load_w1(0, 0)
@@ -164,7 +171,7 @@ def tile_list_paged_skip_adapter_kernel(
                 lhsT=codes[key][:, t * P : (t + 1) * P].bitcast(FP8X4),
                 lhsT_scale=scales[key][:, t * P : (t + 1) * P],
                 rhs=v_words[a][:, cols].bitcast(FP8X4),
-                rhs_scale=v_scales[4 * a :, cols],
+                rhs_scale=v_scales[a][:, cols],
                 start=(a == order[0]),
                 stop=(a == order[-1]),
             )
@@ -185,13 +192,12 @@ def tile_list_paged_skip_adapter_kernel(
 
         def skip_pass(a, s, u):
             cols = slice(s * HALF, (s + 1) * HALF)
-            low = v_scales[:] if a == 0 else v_scales_low[:].bitcast(U8)
             nc.tensor.matmul_mx(
                 y_bank(s, u)[:],
                 lhsT=skip_words[:, a, 2 * u * P : 2 * (u + 1) * P].bitcast(FP4X4),
                 lhsT_scale=skip_scales[:, a, u * P : (u + 1) * P],
                 rhs=v_words[a][:, cols].bitcast(FP8X4),
-                rhs_scale=low[:, cols],
+                rhs_scale=v_scales[a][:, cols],
                 start=(a == 0),
                 stop=False,
             )
@@ -219,15 +225,17 @@ def tile_list_paged_skip_adapter_kernel(
             picks = offsets[:, first // 16 : last // 16]
             nc.vector.tensor_copy(v_words[a][:, first:last], table[a][:].bitcast(U32).indirect(picks))
 
+        def gather_scales(a):
+            nc.vector.tensor_copy(v_scales[a][:], table_scales[:, a, :].bitcast(U8).indirect(offsets[:]))
+
+        gather_scales(0)
         gather_words(0, 0, S)
-        nc.vector.tensor_copy(v_scales[:], table_scales[:].bitcast(U8).indirect(offsets[:]))
+        gather_scales(1)
         prepare(("w1", 0, 0), "S", 0)
         prepare(("w1", 0, 1), "SV", 1)
         for s in range(HALVES):
             gather_words(1, s * HALF, (s + 1) * HALF)
         load_skip()
-        for q in range(QUADRANTS):
-            nc.sync.dma_start(v_scales_low[32 * q : 32 * q + 4, :], v_scales[32 * q + 4 : 32 * q + 8, :].bitcast(I32))
         load_w1(2, 0)
         load_w1(2, 1)
         load_w2(0)

@@ -64,8 +64,8 @@ def tile_list_paged_skip_adapter_kernel(
 
         nc.vector.memset(table_scales[:, 0, :], 0)
         nc.gpsimd.memset(table_scales[:, 1, :], 0)
-        nc.vector.memset(skip_scales[:].bitcast(I32), 0)
         nc.vector.memset(bias_rows[:], 0.0)
+        nc.vector.memset(skip_scales[:].bitcast(I32), 0)
         make_identity(nc, identity[:])
 
         def load_table(a, first=0, last=T):
@@ -80,10 +80,9 @@ def tile_list_paged_skip_adapter_kernel(
             rows = w2[b * K_PASS : (b + 1) * K_PASS, :]
             nc.sync.dma_start(planes[("w2", b)][:], rows.rearrange("(p j) c -> p j c", j=PACK))
 
-        def load_skip_scales(q):
+        def load_skip_scales(r):
             nc.sync.dma_start(
-                skip_scales[32 * q : 32 * q + 4, :, :].bitcast(I32),
-                ws_scales[:, 4 * q : 4 * q + 4, :].rearrange("a r c -> r a c").bitcast(I32),
+                skip_scales[r:P:32, :, :].bitcast(I32), ws_scales[:, r::4, :].rearrange("a q c -> q a c").bitcast(I32)
             )
 
         def load_skip():
@@ -91,17 +90,13 @@ def tile_list_paged_skip_adapter_kernel(
 
         nc.sync.dma_start(offsets[:], offs)
         load_table(0, 0, 3 * T // 8)
-        for q in (0, 2, 1, 3):
+        for r in range(4):
             nc.sync.dma_start(
-                table_scales[32 * q : 32 * q + 4, :, :],
-                tab_scales[:, 4 * q : 4 * q + 4, :].rearrange("a r c -> r a c").bitcast(I32),
+                table_scales[r:P:32, :, :], tab_scales[:, r::4, :].rearrange("a q c -> q a c").bitcast(I32)
             )
-        for q in (0, 2, 1):
-            load_skip_scales(q)
-        load_table(0, 3 * T // 8, T)
-        load_skip_scales(3)
         nc.sync.dma_start(bias_rows[0 : 4 * HP : 4, :], b1.rearrange("(b c) -> b c", b=HP))
         nc.sync.dma_start(bias_rows[4 * HP : 4 * HP + 1, :], b2.rearrange("(o c) -> o c", o=1))
+        load_table(0, 3 * T // 8, T)
         load_w1(0, 0)
         load_w1(0, 1)
         load_table(1)
@@ -235,6 +230,8 @@ def tile_list_paged_skip_adapter_kernel(
         prepare(("w1", 0, 1), "SV", 1)
         for s in range(HALVES):
             gather_words(1, s * HALF, (s + 1) * HALF)
+        for r in range(4):
+            load_skip_scales(r)
         load_skip()
         load_w1(2, 0)
         load_w1(2, 1)

@@ -22,12 +22,13 @@ PACK = 4
 K_PASS = P * PACK
 HALF = 512
 HALVES = S // HALF
-KP = K // K_PASS
-HP = H // K_PASS
-NT = N // P
-QUADRANTS = 4
-BANKS = 8
-STAGING = 4
+K_PASSES = K // K_PASS
+H_BLOCKS = H // K_PASS
+OUT_TILES = N // P
+QUADRANT = 32
+SCALE_ROWS = 4
+BIAS_STEP = 4
+TABLE_HEAD = 3 * T // 8
 
 
 def tile_list_paged_skip_adapter_kernel(
@@ -39,28 +40,33 @@ def tile_list_paged_skip_adapter_kernel(
         psum = ctx.enter_context(tc.psum_pool(name="psum", bufs=1))
 
         offsets = keep.tile([P, S // 16], U16, name="offsets")
-        table = [keep.tile([P, T], I32, name=f"table{a}", align_bytes=64) for a in range(KP)]
-        table_scales = keep.tile([P, KP, T // 4], I32, name="table_scales", align_bytes=64)
-        v_words = [keep.tile([P, S], U32, name=f"v_words{a}", align_bytes=64) for a in range(KP)]
-        v_scales = [keep.tile([P, S], U8, name=f"v_scales{a}", align_bytes=64) for a in range(KP)]
-        skip_words = keep.tile([P, KP, 2 * N], U8, name="skip_words", align_bytes=64)
-        skip_scales = keep.tile([P, KP, N], U8, name="skip_scales", align_bytes=64)
+        table = [keep.tile([P, T], I32, name=f"table{a}", align_bytes=64) for a in range(K_PASSES)]
+        table_scales = keep.tile([P, K_PASSES, T // 4], I32, name="table_scales", align_bytes=64)
+        v_words = [keep.tile([P, S], U32, name=f"v_words{a}", align_bytes=64) for a in range(K_PASSES)]
+        v_scales = [keep.tile([P, S], U8, name=f"v_scales{a}", align_bytes=64) for a in range(K_PASSES)]
+        skip_words = keep.tile([P, K_PASSES, 2 * N], U8, name="skip_words", align_bytes=64)
+        skip_scales = keep.tile([P, K_PASSES, N], U8, name="skip_scales", align_bytes=64)
         bias_rows = keep.tile([P, K_PASS], F32, name="bias_rows")
         identity = keep.tile([P, P], F32, name="identity")
-        b1_cols = keep.tile([P, PACK, HP], F32, name="b1_cols")
-        b2_cols = keep.tile([P, NT], F32, name="b2_cols")
-        w1_keys = [("w1", b, a) for b in range(HP) for a in range(KP)]
-        w2_keys = [("w2", b) for b in range(HP)]
-        h_keys = [("h", b, s) for b in range(HP) for s in range(HALVES)]
+        b1_cols = keep.tile([P, PACK, H_BLOCKS], F32, name="b1_cols")
+        b2_cols = keep.tile([P, OUT_TILES], F32, name="b2_cols")
+
+        w1_keys = [("w1", b, a) for b in range(H_BLOCKS) for a in range(K_PASSES)]
+        w2_keys = [("w2", b) for b in range(H_BLOCKS)]
+        h_keys = [("h", b, s) for b in range(H_BLOCKS) for s in range(HALVES)]
+        late_codes = ("h", 1, 0)
         planes, codes, scales = {}, {}, {}
         for key in w1_keys + w2_keys + h_keys:
             label = "".join(str(part) for part in key)
             dtype = BF16 if key[0] == "h" else F32
             planes[key] = keep.tile([P, PACK, K_PASS], dtype, name="planes_" + label, align_bytes=64)
-            codes[key] = keep.tile([P, K_PASS], U32, name="codes_" + label, align_bytes=64)
+            if key != late_codes:
+                codes[key] = keep.tile([P, K_PASS], U32, name="codes_" + label, align_bytes=64)
             scales[key] = keep.tile([P, K_PASS], U8, name="scales_" + label, align_bytes=64)
-        staging = [keep.tile([P, K_PASS * PACK], BF16, name=f"staging{n}", align_bytes=64) for n in range(STAGING)]
-        banks = [psum.tile([P, HALF], F32, name=f"bank{n}") for n in range(BANKS)]
+
+        staging = [keep.tile([P, K_PASS * PACK], BF16, name=f"staging{n}", align_bytes=64) for n in range(4)]
+        even, odd, scalar_first, scalar_last = staging
+        banks = [psum.tile([P, HALF], F32, name=f"bank{n}") for n in range(HALVES * OUT_TILES)]
 
         nc.vector.memset(table_scales[:, 0, :], 0)
         nc.gpsimd.memset(table_scales[:, 1, :], 0)
@@ -68,122 +74,109 @@ def tile_list_paged_skip_adapter_kernel(
         nc.vector.memset(skip_scales[:].bitcast(I32), 0)
         make_identity(nc, identity[:])
 
-        def load_table(a, first=0, last=T):
+        def load_table(a, first, last):
             words = tab_words[a].rearrange("p t i -> p (t i)").bitcast(I32)
             nc.sync.dma_start(table[a][:, first:last], words[:, first:last])
 
-        def load_w1(b, a, first=0, last=K_PASS):
-            rows = w1[a * K_PASS : (a + 1) * K_PASS, b * K_PASS + first : b * K_PASS + last]
-            nc.sync.dma_start(planes[("w1", b, a)][:, :, first:last], rows.rearrange("(p j) c -> p j c", j=PACK))
+        def load_scale_rows(tile, source):
+            for r in range(SCALE_ROWS):
+                rows = source[:, r::SCALE_ROWS, :].rearrange("a q c -> q a c")
+                nc.sync.dma_start(tile[r:P:QUADRANT, :, :], rows.bitcast(I32))
+
+        def load_w1(b, a):
+            rows = w1[a * K_PASS : (a + 1) * K_PASS, b * K_PASS : (b + 1) * K_PASS]
+            nc.sync.dma_start(planes[("w1", b, a)][:], rows.rearrange("(p j) c -> p j c", j=PACK))
 
         def load_w2(b):
             rows = w2[b * K_PASS : (b + 1) * K_PASS, :]
             nc.sync.dma_start(planes[("w2", b)][:], rows.rearrange("(p j) c -> p j c", j=PACK))
 
-        def load_skip_scales(r):
-            nc.sync.dma_start(
-                skip_scales[r:P:32, :, :].bitcast(I32), ws_scales[:, r::4, :].rearrange("a q c -> q a c").bitcast(I32)
-            )
-
-        def load_skip():
-            nc.sync.dma_start(skip_words[:].bitcast(I32), ws_words.rearrange("a p c -> p a c").bitcast(I32))
-
+        b2_row = BIAS_STEP * H_BLOCKS
         nc.sync.dma_start(offsets[:], offs)
-        load_table(0, 0, 3 * T // 8)
-        for r in range(4):
-            nc.sync.dma_start(
-                table_scales[r:P:32, :, :], tab_scales[:, r::4, :].rearrange("a q c -> q a c").bitcast(I32)
-            )
-        nc.sync.dma_start(bias_rows[0 : 4 * HP : 4, :], b1.rearrange("(b c) -> b c", b=HP))
-        nc.sync.dma_start(bias_rows[4 * HP : 4 * HP + 1, :], b2.rearrange("(o c) -> o c", o=1))
-        load_table(0, 3 * T // 8, T)
-        load_w1(0, 0)
-        load_w1(0, 1)
-        load_table(1)
-        for a in range(KP):
+        load_table(0, 0, TABLE_HEAD)
+        load_scale_rows(table_scales, tab_scales)
+        nc.sync.dma_start(bias_rows[0:b2_row:BIAS_STEP, :], b1.rearrange("(b c) -> b c", b=H_BLOCKS))
+        nc.sync.dma_start(bias_rows[b2_row : b2_row + 1, :], b2.rearrange("(o c) -> o c", o=1))
+        load_table(0, TABLE_HEAD, T)
+        for a in range(K_PASSES):
+            load_w1(0, a)
+        load_table(1, 0, T)
+        for a in range(K_PASSES):
             load_w1(1, a)
 
         for t in range(PACK):
-            nc.tensor.transpose(banks[6][:, t * P : (t + 1) * P], bias_rows[:, t::PACK], identity[:])
-        for u in range(NT):
-            nc.tensor.transpose(banks[7][:, u * P : (u + 1) * P], bias_rows[:, u * P : (u + 1) * P], identity[:])
-        nc.scalar.copy(out=b1_cols[:], in_=banks[6][:].rearrange("p (t r) -> p t r", t=PACK)[:, :, 0 : 4 * HP : 4])
-        nc.scalar.copy(out=b2_cols[:], in_=banks[7][:].rearrange("p (u r) -> p u r", u=NT)[:, :, 4 * HP])
+            nc.tensor.transpose(banks[-2][:, t * P : (t + 1) * P], bias_rows[:, t::PACK], identity[:])
+        for u in range(OUT_TILES):
+            nc.tensor.transpose(banks[-1][:, u * P : (u + 1) * P], bias_rows[:, u * P : (u + 1) * P], identity[:])
+        nc.scalar.copy(out=b1_cols[:], in_=banks[-2][:].rearrange("p (t r) -> p t r", t=PACK)[:, :, 0:b2_row:BIAS_STEP])
+        nc.scalar.copy(out=b2_cols[:], in_=banks[-1][:].rearrange("p (u r) -> p u r", u=OUT_TILES)[:, :, b2_row])
 
         staged = {}
 
-        def interleave(key, engines, slot):
-            tile = staging[slot]
+        def interleave(key, tile, copies):
             staged[key] = tile
             if key[0] == "w1":
                 dst = tile[:].rearrange("p (t m h j) -> p m j h t", t=PACK, h=2, j=PACK)
                 src = planes[key][:].rearrange("p j (m h t) -> p m j h t", h=2, t=PACK)
+                width = PACK // len(copies)
+                for n, copy in enumerate(copies):
+                    share = slice(n * width, (n + 1) * width)
+                    copy(out=dst[:, :, :, :, share], in_=src[:, :, :, :, share])
             else:
                 dst = tile[:].rearrange("p (m i j) -> p m j i", i=PACK, j=PACK)
                 src = planes[key][:].rearrange("p j (m i) -> p m j i", i=PACK)
-            for n, engine in enumerate(engines):
-                if key[0] == "w1":
-                    width = PACK // len(engines)
-                    part = (slice(None), slice(None), slice(None), slice(None), slice(n * width, (n + 1) * width))
-                else:
-                    width = P // len(engines)
-                    part = (slice(None), slice(n * width, (n + 1) * width))
-                if engine == "V":
-                    nc.vector.tensor_copy(out=dst[part], in_=src[part])
-                else:
-                    nc.scalar.copy(out=dst[part], in_=src[part])
+                width = P // len(copies)
+                for n, copy in enumerate(copies):
+                    share = slice(n * width, (n + 1) * width)
+                    copy(out=dst[:, share], in_=src[:, share])
 
-        def quantise(key):
-            nc.vector.quantize_mx(out=codes[key][:].bitcast(FP8X4), scales=scales[key][:], in_=staged[key][:])
-
-        def prepare_w1(key, slot):
-            tile = staging[slot]
-            dst = tile[:].rearrange("p (t m h j) -> p m j h t", t=PACK, h=2, j=PACK)
-            src = planes[key][:].rearrange("p j (m h t) -> p m j h t", h=2, t=PACK)
-            for pair in range(2):
-                part = slice(2 * pair, 2 * pair + 2)
-                nc.vector.tensor_copy(out=dst[:, :, :, :, part], in_=src[:, :, :, :, part])
-            for pair in range(2):
-                part = slice(2 * pair * P, 2 * (pair + 1) * P)
+        def quantise(key, parts=1):
+            width = K_PASS // parts
+            for first in range(0, K_PASS, width):
                 nc.vector.quantize_mx(
-                    out=codes[key][:, part].bitcast(FP8X4),
-                    scales=scales[key][:, part],
-                    in_=tile[:, PACK * part.start : PACK * part.stop],
+                    out=codes[key][:, first : first + width].bitcast(FP8X4),
+                    scales=scales[key][:, first : first + width],
+                    in_=staged[key][:, PACK * first : PACK * (first + width)],
                 )
 
-        def prepare(key, engines, slot):
-            interleave(key, engines, slot)
+        on_vector, on_scalar = nc.vector.tensor_copy, nc.scalar.copy
+
+        def prepare(key, tile, copies):
+            interleave(key, tile, copies)
             quantise(key)
 
-        def h_bank(b, s, t):
-            return banks[NT * s + t] if b + 1 < HP else banks[NT + t]
+        def prepare_in_two(key, tile):
+            interleave(key, tile, [on_vector, on_vector])
+            quantise(key, parts=2)
 
-        def hidden_pass(b, s, t, a, order):
-            cols = slice(s * HALF, (s + 1) * HALF)
-            key = ("w1", b, a)
-            nc.tensor.matmul_mx(
-                h_bank(b, s, t)[:],
-                lhsT=codes[key][:, t * P : (t + 1) * P].bitcast(FP8X4),
-                lhsT_scale=scales[key][:, t * P : (t + 1) * P],
-                rhs=v_words[a][:, cols].bitcast(FP8X4),
-                rhs_scale=v_scales[a][:, cols],
-                start=(a == order[0]),
-                stop=(a == order[-1]),
-            )
+        def gather_words(a, first, last):
+            picks = offsets[:, first // 16 : last // 16]
+            nc.vector.tensor_copy(v_words[a][:, first:last], table[a][:].bitcast(U32).indirect(picks))
+
+        def gather_scales(a):
+            nc.vector.tensor_copy(v_scales[a][:], table_scales[:, a, :].bitcast(U8).indirect(offsets[:]))
 
         def hidden(b, s):
-            order = list(range(KP))
-            if HALVES * b + s > 2:
-                order = order[::-1]
+            cols = slice(s * HALF, (s + 1) * HALF)
+            lower = s == 0 and b + 1 < H_BLOCKS
+            order = range(K_PASSES) if lower else range(K_PASSES)[::-1]
             for t in range(PACK):
+                bank = banks[t if lower else OUT_TILES + t]
                 for a in order:
-                    hidden_pass(b, s, t, a, order)
-                nc.scalar.activation(
-                    planes[("h", b, s)][:, t, :], h_bank(b, s, t)[:], ACT.Relu, bias=b1_cols[:, t, b : b + 1]
-                )
+                    key = ("w1", b, a)
+                    nc.tensor.matmul_mx(
+                        bank[:],
+                        lhsT=codes[key][:, t * P : (t + 1) * P].bitcast(FP8X4),
+                        lhsT_scale=scales[key][:, t * P : (t + 1) * P],
+                        rhs=v_words[a][:, cols].bitcast(FP8X4),
+                        rhs_scale=v_scales[a][:, cols],
+                        start=(a == order[0]),
+                        stop=(a == order[-1]),
+                    )
+                nc.scalar.activation(planes[("h", b, s)][:, t, :], bank[:], ACT.Relu, bias=b1_cols[:, t, b : b + 1])
 
         def y_bank(s, u):
-            return banks[NT * s + u]
+            return banks[OUT_TILES * s + u]
 
         def skip_pass(a, s, u):
             cols = slice(s * HALF, (s + 1) * HALF)
@@ -208,65 +201,65 @@ def tile_list_paged_skip_adapter_kernel(
                 stop=last,
             )
 
-        def finish(s, u, engine):
+        def finish(s, u, by_scalar):
             result = keep.tile([P, HALF], F32, name=f"result{s}{u}")
-            if engine == "S":
+            if by_scalar:
                 nc.scalar.activation(result[:], y_bank(s, u)[:], ACT.Identity, bias=b2_cols[:, u : u + 1])
             else:
                 nc.vector.tensor_scalar(result[:], y_bank(s, u)[:], b2_cols[:, u : u + 1], None, op0=ALU.add)
             nc.sync.dma_start(out[u * P : (u + 1) * P, s * HALF : (s + 1) * HALF], result[:])
 
-        def gather_words(a, first, last):
-            picks = offsets[:, first // 16 : last // 16]
-            nc.vector.tensor_copy(v_words[a][:, first:last], table[a][:].bitcast(U32).indirect(picks))
-
-        def gather_scales(a):
-            nc.vector.tensor_copy(v_scales[a][:], table_scales[:, a, :].bitcast(U8).indirect(offsets[:]))
-
         gather_scales(0)
         gather_words(0, 0, S)
         gather_scales(1)
-        prepare(("w1", 0, 0), "S", 0)
-        prepare(("w1", 0, 1), "SV", 1)
+        prepare(("w1", 0, 0), even, [on_scalar])
+        prepare(("w1", 0, 1), odd, [on_scalar, on_vector])
         for s in range(HALVES):
             gather_words(1, s * HALF, (s + 1) * HALF)
-        for r in range(4):
-            load_skip_scales(r)
-        load_skip()
-        load_w1(2, 0)
-        load_w1(2, 1)
-        load_w2(0)
-        load_w2(1)
-        load_w2(2)
 
-        for b in range(HP - 1):
-            for s in range(HALVES):
-                hidden(b, s)
-            for a in range(KP):
-                prepare_w1(("w1", b + 1, a), a)
-            prepare(("h", b, 0), "V" if b == 0 else "SV", 1)
-        for a in range(KP):
-            for u in range(NT):
+        load_scale_rows(skip_scales[:].bitcast(I32), ws_scales)
+        nc.sync.dma_start(skip_words[:].bitcast(I32), ws_words.rearrange("a p c -> p a c").bitcast(I32))
+        for a in range(K_PASSES):
+            load_w1(2, a)
+        for b in range(H_BLOCKS):
+            load_w2(b)
+
+        for s in range(HALVES):
+            hidden(0, s)
+        prepare_in_two(("w1", 1, 0), even)
+        prepare_in_two(("w1", 1, 1), odd)
+        prepare_in_two(("h", 0, 0), odd)
+        for s in range(HALVES):
+            hidden(1, s)
+        interleave(("h", 1, 0), scalar_first, [on_scalar])
+        prepare_in_two(("w1", 2, 0), even)
+        prepare_in_two(("w1", 2, 1), odd)
+        for a in range(K_PASSES):
+            for u in range(OUT_TILES):
                 skip_pass(a, 0, u)
         for s in range(HALVES):
-            hidden(HP - 1, s)
+            hidden(2, s)
 
-        for b in range(HP):
-            if b == HP - 1:
-                prepare(("h", b, 0), "V", 2)
-            prepare(("w2", b), "V", b % 2)
-            for u in range(NT):
-                main_pass(b, 0, u, b == HP - 1)
-        for u in range(NT):
-            finish(0, u, "S")
-        prepare(("h", 2, 1), "S", 3)
-        prepare(("h", 0, 1), "V", 2)
-        prepare(("h", 1, 1), "S", 1)
-        for u in range(NT):
-            for a in range(KP):
+        prepare_in_two(("w2", 0), even)
+        codes[late_codes] = keep.tile([P, K_PASS], U32, name="codes_h10", tag="planes_w20", align_bytes=64)
+        quantise(late_codes)
+        prepare_in_two(("w2", 1), odd)
+        prepare_in_two(("w2", 2), even)
+        prepare(("h", 2, 0), odd, [on_vector])
+        for b in range(H_BLOCKS):
+            for u in range(OUT_TILES):
+                main_pass(b, 0, u, last=(b == H_BLOCKS - 1))
+        for u in range(OUT_TILES):
+            finish(0, u, by_scalar=True)
+
+        prepare(("h", 1, 1), scalar_first, [on_scalar])
+        prepare(("h", 2, 1), scalar_last, [on_scalar])
+        prepare(("h", 0, 1), even, [on_vector])
+        for u in range(OUT_TILES):
+            for a in range(K_PASSES):
                 skip_pass(a, 1, u)
-            main_pass(2, 1, u, False)
-        for u in range(NT):
-            main_pass(0, 1, u, False)
-            main_pass(1, 1, u, True)
-            finish(1, u, "SV"[u % 2])
+            main_pass(1, 1, u, last=False)
+        for u in range(OUT_TILES):
+            main_pass(2, 1, u, last=False)
+            main_pass(0, 1, u, last=True)
+            finish(1, u, by_scalar=(u % 2 == 0))

@@ -41,9 +41,10 @@ def tile_list_paged_skip_adapter_kernel(
 
         offsets = keep.tile([P, S // 16], U16, name="offsets")
         table = [keep.tile([P, T], I32, name=f"table{a}", align_bytes=64) for a in range(K_PASSES)]
-        table_scales = keep.tile([P, K_PASSES, T // 4], I32, name="table_scales", align_bytes=64)
+        table_scales = keep.tile([P, T // 4], I32, name="table_scales", align_bytes=64)
+        picked_scales = keep.tile([P, S], U8, name="picked_scales", align_bytes=64)
         v_words = [keep.tile([P, S], U32, name=f"v_words{a}", align_bytes=64) for a in range(K_PASSES)]
-        v_scales = [keep.tile([P, S], U8, name=f"v_scales{a}", align_bytes=64) for a in range(K_PASSES)]
+        v_scales = keep.tile([P, K_PASSES, S], U8, name="v_scales", align_bytes=64)
         skip_words = keep.tile([P, K_PASSES, 2 * N], U8, name="skip_words", align_bytes=64)
         skip_scales = keep.tile([P, K_PASSES, N], U8, name="skip_scales", align_bytes=64)
         bias_rows = keep.tile([P, K_PASS], F32, name="bias_rows")
@@ -68,20 +69,16 @@ def tile_list_paged_skip_adapter_kernel(
         even, odd, scalar_first, scalar_last = staging
         banks = [psum.tile([P, HALF], F32, name=f"bank{n}") for n in range(HALVES * OUT_TILES)]
 
-        nc.vector.memset(table_scales[:, 0, :], 0)
-        nc.gpsimd.memset(table_scales[:, 1, :], 0)
+        nc.vector.memset(table_scales[:, : T // 8], 0)
+        nc.gpsimd.memset(table_scales[:, T // 8 :], 0)
         nc.vector.memset(bias_rows[:], 0.0)
+        nc.vector.memset(v_scales[:].bitcast(I32), 0)
         nc.vector.memset(skip_scales[:].bitcast(I32), 0)
         make_identity(nc, identity[:])
 
         def load_table(a, first, last):
             words = tab_words[a].rearrange("p t i -> p (t i)").bitcast(I32)
             nc.sync.dma_start(table[a][:, first:last], words[:, first:last])
-
-        def load_scale_rows(tile, source):
-            for r in range(SCALE_ROWS):
-                rows = source[:, r::SCALE_ROWS, :].rearrange("a q c -> q a c")
-                nc.sync.dma_start(tile[r:P:QUADRANT, :, :], rows.bitcast(I32))
 
         def load_w1(b, a):
             rows = w1[a * K_PASS : (a + 1) * K_PASS, b * K_PASS : (b + 1) * K_PASS]
@@ -94,12 +91,20 @@ def tile_list_paged_skip_adapter_kernel(
         b2_row = BIAS_STEP * H_BLOCKS
         nc.sync.dma_start(offsets[:], offs)
         load_table(0, 0, TABLE_HEAD)
-        load_scale_rows(table_scales, tab_scales)
+        for a in range(K_PASSES):
+            nc.sync.dma_start(table_scales[a:QUADRANT:K_PASSES, :], tab_scales[a].bitcast(I32))
         nc.sync.dma_start(bias_rows[0:b2_row:BIAS_STEP, :], b1.rearrange("(b c) -> b c", b=H_BLOCKS))
         nc.sync.dma_start(bias_rows[b2_row : b2_row + 1, :], b2.rearrange("(o c) -> o c", o=1))
         load_table(0, TABLE_HEAD, T)
-        for a in range(K_PASSES):
-            load_w1(0, a)
+        load_w1(0, 0)
+        nc.vector.tensor_copy(picked_scales[:], table_scales[:].bitcast(U8).indirect(offsets[:]))
+        picked_rows = K_PASSES * SCALE_ROWS
+        for q in (0, 2, 1, 3):
+            nc.sync.dma_start(
+                v_scales[QUADRANT * q : QUADRANT * q + SCALE_ROWS].bitcast(I32),
+                picked_scales[picked_rows * q : picked_rows * (q + 1), :].bitcast(I32),
+            )
+        load_w1(0, 1)
         load_table(1, 0, T)
         for a in range(K_PASSES):
             load_w1(1, a)
@@ -153,9 +158,6 @@ def tile_list_paged_skip_adapter_kernel(
             picks = offsets[:, first // 16 : last // 16]
             nc.vector.tensor_copy(v_words[a][:, first:last], table[a][:].bitcast(U32).indirect(picks))
 
-        def gather_scales(a):
-            nc.vector.tensor_copy(v_scales[a][:], table_scales[:, a, :].bitcast(U8).indirect(offsets[:]))
-
         def hidden(b, s):
             cols = slice(s * HALF, (s + 1) * HALF)
             lower = s == 0 and b + 1 < H_BLOCKS
@@ -169,7 +171,7 @@ def tile_list_paged_skip_adapter_kernel(
                         lhsT=codes[key][:, t * P : (t + 1) * P].bitcast(FP8X4),
                         lhsT_scale=scales[key][:, t * P : (t + 1) * P],
                         rhs=v_words[a][:, cols].bitcast(FP8X4),
-                        rhs_scale=v_scales[a][:, cols],
+                        rhs_scale=v_scales[:, a, cols],
                         start=(a == order[0]),
                         stop=(a == order[-1]),
                     )
@@ -185,7 +187,7 @@ def tile_list_paged_skip_adapter_kernel(
                 lhsT=skip_words[:, a, 2 * u * P : 2 * (u + 1) * P].bitcast(FP4X4),
                 lhsT_scale=skip_scales[:, a, u * P : (u + 1) * P],
                 rhs=v_words[a][:, cols].bitcast(FP8X4),
-                rhs_scale=v_scales[a][:, cols],
+                rhs_scale=v_scales[:, a, cols],
                 start=(a == 0),
                 stop=False,
             )
@@ -209,15 +211,15 @@ def tile_list_paged_skip_adapter_kernel(
                 nc.vector.tensor_scalar(result[:], y_bank(s, u)[:], b2_cols[:, u : u + 1], None, op0=ALU.add)
             nc.sync.dma_start(out[u * P : (u + 1) * P, s * HALF : (s + 1) * HALF], result[:])
 
-        gather_scales(0)
         gather_words(0, 0, S)
-        gather_scales(1)
         prepare(("w1", 0, 0), even, [on_scalar])
         prepare(("w1", 0, 1), odd, [on_scalar, on_vector])
         for s in range(HALVES):
             gather_words(1, s * HALF, (s + 1) * HALF)
 
-        load_scale_rows(skip_scales[:].bitcast(I32), ws_scales)
+        for r in range(SCALE_ROWS):
+            rows = ws_scales[:, r::SCALE_ROWS, :].rearrange("a q c -> q a c")
+            nc.sync.dma_start(skip_scales[:].bitcast(I32)[r:P:QUADRANT, :, :], rows.bitcast(I32))
         nc.sync.dma_start(skip_words[:].bitcast(I32), ws_words.rearrange("a p c -> p a c").bitcast(I32))
         for a in range(K_PASSES):
             load_w1(2, a)

@@ -21,14 +21,15 @@ P = 128
 PACK = 4
 K_PASS = P * PACK
 HALF = 512
+QUARTER = HALF // 2
 HALVES = S // HALF
 K_PASSES = K // K_PASS
 H_BLOCKS = H // K_PASS
 OUT_TILES = N // P
 QUADRANT = 32
 SCALE_ROWS = 4
-BIAS_STEP = 4
 TABLE_HEAD = 3 * T // 8
+BIAS_STEP = 4
 
 
 def tile_list_paged_skip_adapter_kernel(
@@ -55,18 +56,22 @@ def tile_list_paged_skip_adapter_kernel(
         w1_keys = [("w1", b, a) for b in range(H_BLOCKS) for a in range(K_PASSES)]
         w2_keys = [("w2", b) for b in range(H_BLOCKS)]
         h_keys = [("h", b, s) for b in range(H_BLOCKS) for s in range(HALVES)]
-        late_codes = ("h", 1, 0)
+        late_codes = [("h", 0, 0), ("h", 1, 0), ("h", 2, 0), ("h", 2, 1)]
         planes, codes, scales = {}, {}, {}
         for key in w1_keys + w2_keys + h_keys:
             label = "".join(str(part) for part in key)
             dtype = BF16 if key[0] == "h" else F32
             planes[key] = keep.tile([P, PACK, K_PASS], dtype, name="planes_" + label, align_bytes=64)
-            if key != late_codes:
+            if key not in late_codes:
                 codes[key] = keep.tile([P, K_PASS], U32, name="codes_" + label, align_bytes=64)
             scales[key] = keep.tile([P, K_PASS], U8, name="scales_" + label, align_bytes=64)
 
-        staging = [keep.tile([P, K_PASS * PACK], BF16, name=f"staging{n}", align_bytes=64) for n in range(4)]
-        even, odd, scalar_first, scalar_last = staging
+        staging = [keep.tile([P, K_PASS * PACK], BF16, name=f"staging{n}", align_bytes=64) for n in range(2)]
+        even, odd = staging
+
+        def on_bytes_of(tag, name, width, dtype):
+            return keep.tile([P, width], dtype, name=name, tag=tag, align_bytes=64)
+
         banks = [psum.tile([P, HALF], F32, name=f"bank{n}") for n in range(HALVES * OUT_TILES)]
 
         nc.vector.memset(table_scales[:, : T // 8], 0)
@@ -117,103 +122,118 @@ def tile_list_paged_skip_adapter_kernel(
         nc.scalar.copy(out=b2_cols[:], in_=banks[-1][:].rearrange("p (u r) -> p u r", u=OUT_TILES)[:, :, b2_row])
 
         staged = {}
-
-        def interleave(key, tile, copies):
-            staged[key] = tile
-            if key[0] == "w1":
-                dst = tile[:].rearrange("p (t m h j) -> p m j h t", t=PACK, h=2, j=PACK)
-                src = planes[key][:].rearrange("p j (m h t) -> p m j h t", h=2, t=PACK)
-                width = PACK // len(copies)
-                for n, copy in enumerate(copies):
-                    share = slice(n * width, (n + 1) * width)
-                    copy(out=dst[:, :, :, :, share], in_=src[:, :, :, :, share])
-            else:
-                dst = tile[:].rearrange("p (m i j) -> p m j i", i=PACK, j=PACK)
-                src = planes[key][:].rearrange("p j (m i) -> p m j i", i=PACK)
-                width = P // len(copies)
-                for n, copy in enumerate(copies):
-                    share = slice(n * width, (n + 1) * width)
-                    copy(out=dst[:, share], in_=src[:, share])
-
-        def quantise(key, parts=1):
-            width = K_PASS // parts
-            for first in range(0, K_PASS, width):
-                nc.vector.quantize_mx(
-                    out=codes[key][:, first : first + width].bitcast(FP8X4),
-                    scales=scales[key][:, first : first + width],
-                    in_=staged[key][:, PACK * first : PACK * (first + width)],
-                )
-
         on_vector, on_scalar = nc.vector.tensor_copy, nc.scalar.copy
+        FIRST, SECOND, WHOLE = (0, 2), (2, 4), (0, 4)
 
-        def prepare(key, tile, copies):
-            interleave(key, tile, copies)
-            quantise(key)
+        def interleave(copy, key, share, tile, at=None):
+            first, last = share
+            at = first if at is None else at
+            room = tile[:, at * K_PASS : (at + last - first) * K_PASS]
+            for n in range(first, last):
+                staged[key, n] = (tile, at + n - first)
+            if key[0] == "w1":
+                dst = room.rearrange("p (t m h j) -> p m j h t", t=last - first, h=2, j=PACK)
+                src = planes[key][:].rearrange("p j (m h t) -> p m j h t", h=2, t=PACK)[:, :, :, :, first:last]
+            else:
+                dst = room.rearrange("p (m i j) -> p m j i", i=PACK, j=PACK)
+                src = planes[key][:, :, first * P : last * P].rearrange("p j (m i) -> p m j i", i=PACK)
+            copy(out=dst, in_=src)
+
+        def quantise(key, share):
+            first, last = share
+            tile, at = staged[key, first]
+            nc.vector.quantize_mx(
+                out=codes[key][:, first * P : last * P].bitcast(FP8X4),
+                scales=scales[key][:, first * P : last * P],
+                in_=tile[:, at * K_PASS : (at + last - first) * K_PASS],
+            )
 
         def prepare_in_two(key, tile):
-            interleave(key, tile, [on_vector, on_vector])
-            quantise(key, parts=2)
+            for share in (FIRST, SECOND):
+                interleave(on_vector, key, share, tile)
+            for share in (FIRST, SECOND):
+                quantise(key, share)
 
         def gather_words(a, first, last):
             picks = offsets[:, first // 16 : last // 16]
             nc.vector.tensor_copy(v_words[a][:, first:last], table[a][:].bitcast(U32).indirect(picks))
 
-        def hidden(b, s):
-            cols = slice(s * HALF, (s + 1) * HALF)
-            lower = s == 0 and b + 1 < H_BLOCKS
-            order = range(K_PASSES) if lower else range(K_PASSES)[::-1]
-            for t in range(PACK):
-                bank = banks[t if lower else OUT_TILES + t]
-                for a in order:
-                    key = ("w1", b, a)
-                    nc.tensor.matmul_mx(
-                        bank[:],
-                        lhsT=codes[key][:, t * P : (t + 1) * P].bitcast(FP8X4),
-                        lhsT_scale=scales[key][:, t * P : (t + 1) * P],
-                        rhs=v_words[a][:, cols].bitcast(FP8X4),
-                        rhs_scale=v_scales[:, a, cols],
-                        start=(a == order[0]),
-                        stop=(a == order[-1]),
-                    )
-                nc.scalar.activation(planes[("h", b, s)][:, t, :], bank[:], ACT.Relu, bias=b1_cols[:, t, b : b + 1])
+        def hidden_bank(b, s, t):
+            return banks[t if s == 0 and b + 1 < H_BLOCKS else OUT_TILES + t]
 
-        def y_bank(s, u):
-            return banks[OUT_TILES * s + u]
-
-        def skip_pass(a, s, u):
+        def hidden_pass(b, s, t, a):
             cols = slice(s * HALF, (s + 1) * HALF)
+            key, bank = ("w1", b, a), hidden_bank(b, s, t)
             nc.tensor.matmul_mx(
-                y_bank(s, u)[:],
-                lhsT=skip_words[:, a, 2 * u * P : 2 * (u + 1) * P].bitcast(FP4X4),
-                lhsT_scale=skip_scales[:, a, u * P : (u + 1) * P],
+                bank[:],
+                lhsT=codes[key][:, t * P : (t + 1) * P].bitcast(FP8X4),
+                lhsT_scale=scales[key][:, t * P : (t + 1) * P],
                 rhs=v_words[a][:, cols].bitcast(FP8X4),
                 rhs_scale=v_scales[:, a, cols],
                 start=(a == 0),
-                stop=False,
+                stop=(a == K_PASSES - 1),
             )
+            if a == K_PASSES - 1:
+                nc.scalar.activation(planes[("h", b, s)][:, t, :], bank[:], ACT.Relu, bias=b1_cols[:, t, b : b + 1])
 
-        def main_pass(b, s, u, last):
-            nc.tensor.matmul_mx(
-                y_bank(s, u)[:],
-                lhsT=codes[("w2", b)][:, u * P : (u + 1) * P].bitcast(FP8X4),
-                lhsT_scale=scales[("w2", b)][:, u * P : (u + 1) * P],
-                rhs=codes[("h", b, s)][:].bitcast(FP8X4),
-                rhs_scale=scales[("h", b, s)][:],
-                start=False,
-                stop=last,
-            )
+        def hidden(b, halves):
+            for a in range(K_PASSES):
+                for s in halves:
+                    for t in range(PACK):
+                        hidden_pass(b, s, t, a)
 
-        def finish(s, u, by_scalar):
-            result = keep.tile([P, HALF], F32, name=f"result{s}{u}")
+        EARLY, MIDDLE, LATE = (0, HALF), (HALF, QUARTER), (HALF + QUARTER, QUARTER)
+
+        def y_tile(group, u):
+            first, width = group
+            place = (first * OUT_TILES + u * width)
+            return banks[place // HALF][:, place % HALF : place % HALF + width]
+
+        def skip_passes(group):
+            first, width = group
+            step = width if width == HALF else P
+            for u in range(OUT_TILES):
+                for a in range(K_PASSES):
+                    for c in range(0, width, step):
+                        cols = slice(first + c, first + c + step)
+                        nc.tensor.matmul_mx(
+                            y_tile(group, u)[:, c : c + step],
+                            lhsT=skip_words[:, a, 2 * u * P : 2 * (u + 1) * P].bitcast(FP4X4),
+                            lhsT_scale=skip_scales[:, a, u * P : (u + 1) * P],
+                            rhs=v_words[a][:, cols].bitcast(FP8X4),
+                            rhs_scale=v_scales[:, a, cols],
+                            start=(a == 0 and c == 0 and u * width % HALF == 0),
+                            stop=False,
+                        )
+
+        def main_passes(b, group, last=False):
+            first, width = group
+            key, cols = ("h", b, first // HALF), slice(first % HALF, first % HALF + width)
+            for u in range(OUT_TILES):
+                nc.tensor.matmul_mx(
+                    y_tile(group, u),
+                    lhsT=codes[("w2", b)][:, u * P : (u + 1) * P].bitcast(FP8X4),
+                    lhsT_scale=scales[("w2", b)][:, u * P : (u + 1) * P],
+                    rhs=codes[key][:, cols].bitcast(FP8X4),
+                    rhs_scale=scales[key][:, cols],
+                    start=False,
+                    stop=(last and (u + 1) * width % HALF == 0),
+                )
+
+        def finish(group, u, by_scalar):
+            first, width = group
+            result = keep.tile([P, width], F32, name=f"result{first}_{u}")
             if by_scalar:
-                nc.scalar.activation(result[:], y_bank(s, u)[:], ACT.Identity, bias=b2_cols[:, u : u + 1])
+                nc.scalar.activation(result[:], y_tile(group, u), ACT.Identity, bias=b2_cols[:, u : u + 1])
             else:
-                nc.vector.tensor_scalar(result[:], y_bank(s, u)[:], b2_cols[:, u : u + 1], None, op0=ALU.add)
-            nc.sync.dma_start(out[u * P : (u + 1) * P, s * HALF : (s + 1) * HALF], result[:])
+                nc.vector.tensor_scalar(result[:], y_tile(group, u), b2_cols[:, u : u + 1], None, op0=ALU.add)
+            nc.sync.dma_start(out[u * P : (u + 1) * P, first : first + width], result[:])
 
         gather_words(0, 0, S)
-        prepare(("w1", 0, 0), even, [on_scalar])
-        prepare(("w1", 0, 1), odd, [on_scalar, on_vector])
+        for a, tile in enumerate((even, odd)):
+            interleave(on_vector, ("w1", 0, a), (0, 3), tile)
+            interleave(on_scalar, ("w1", 0, a), (3, 4), tile)
+            quantise(("w1", 0, a), WHOLE)
         for s in range(HALVES):
             gather_words(1, s * HALF, (s + 1) * HALF)
 
@@ -226,42 +246,81 @@ def tile_list_paged_skip_adapter_kernel(
         for b in range(H_BLOCKS):
             load_w2(b)
 
-        for s in range(HALVES):
-            hidden(0, s)
+        h00, h10, h20, h01, h11, h21 = [("h", b, s) for s in range(HALVES) for b in range(H_BLOCKS)]
+
+        hidden(0, range(HALVES))
         prepare_in_two(("w1", 1, 0), even)
+        room = on_bytes_of("planes_w110", "staged_h00", PACK * HALF, BF16)
+        interleave(on_vector, h00, FIRST, room)
+        interleave(on_scalar, h00, SECOND, room)
         prepare_in_two(("w1", 1, 1), odd)
-        prepare_in_two(("h", 0, 0), odd)
-        for s in range(HALVES):
-            hidden(1, s)
-        interleave(("h", 1, 0), scalar_first, [on_scalar])
-        prepare_in_two(("w1", 2, 0), even)
+
+        hidden(1, range(HALVES))
+        room = on_bytes_of("planes_w111", "staged_h01", PACK * QUARTER, BF16)
+        interleave(on_vector, h01, FIRST, room)
+        interleave(on_vector, ("w1", 2, 0), FIRST, even)
+        quantise(h01, FIRST)
+        interleave(on_vector, ("w1", 2, 0), SECOND, even)
+        quantise(("w1", 2, 0), FIRST)
+        codes[h00] = on_bytes_of("planes_w120", "codes_h00", HALF, U32)
+        quantise(h00, WHOLE)
+        quantise(("w1", 2, 0), SECOND)
         prepare_in_two(("w1", 2, 1), odd)
-        for a in range(K_PASSES):
-            for u in range(OUT_TILES):
-                skip_pass(a, 0, u)
-        for s in range(HALVES):
-            hidden(2, s)
+        room = on_bytes_of("planes_w121", "staged_h10", PACK * HALF, BF16)
+        interleave(on_vector, h10, FIRST, room)
+        interleave(on_scalar, h10, SECOND, room)
+        skip_passes(EARLY)
 
-        prepare_in_two(("w2", 0), even)
-        codes[late_codes] = keep.tile([P, K_PASS], U32, name="codes_h10", tag="planes_w20", align_bytes=64)
-        quantise(late_codes)
-        prepare_in_two(("w2", 1), odd)
-        prepare_in_two(("w2", 2), even)
-        prepare(("h", 2, 0), odd, [on_vector])
-        for b in range(H_BLOCKS):
-            for u in range(OUT_TILES):
-                main_pass(b, 0, u, last=(b == H_BLOCKS - 1))
-        for u in range(OUT_TILES):
-            finish(0, u, by_scalar=True)
-
-        prepare(("h", 1, 1), scalar_first, [on_scalar])
-        prepare(("h", 2, 1), scalar_last, [on_scalar])
-        prepare(("h", 0, 1), even, [on_vector])
-        for u in range(OUT_TILES):
+        hidden(2, [0])
+        for t in range(PACK):
             for a in range(K_PASSES):
-                skip_pass(a, 1, u)
-            main_pass(1, 1, u, last=False)
+                hidden_pass(2, 1, t, a)
+        interleave(on_vector, ("w2", 0), FIRST, even)
+        interleave(on_vector, ("w2", 0), SECOND, even)
+        quantise(("w2", 0), FIRST)
+        codes[h10] = on_bytes_of("planes_w20", "codes_h10", HALF, U32)
+        quantise(h10, WHOLE)
+        quantise(("w2", 0), SECOND)
+        interleave(on_vector, ("w2", 1), FIRST, odd)
+        interleave(on_vector, ("w2", 1), SECOND, odd)
+        quantise(("w2", 1), FIRST)
+        room = on_bytes_of("planes_w21", "staged_h20", PACK * HALF, BF16)
+        interleave(on_vector, h20, FIRST, room)
+        interleave(on_scalar, h20, SECOND, room)
+        quantise(("w2", 1), SECOND)
+        interleave(on_vector, ("w2", 2), FIRST, even)
+        interleave(on_vector, ("w2", 2), SECOND, even)
+        quantise(("w2", 2), FIRST)
+        codes[h20] = on_bytes_of("planes_w22", "codes_h20", HALF, U32)
+        quantise(h20, WHOLE)
+        quantise(("w2", 2), SECOND)
+        main_passes(0, EARLY)
+        main_passes(1, EARLY)
+        skip_passes(MIDDLE)
+        main_passes(2, EARLY, last=True)
+        skip_passes(LATE)
+
+        room = on_bytes_of("staging0", "staged_late", 3 * PACK * QUARTER, BF16)
+        codes[h21] = on_bytes_of("planes_w21", "codes_h21", HALF, U32)
+        interleave(on_scalar, h21, FIRST, odd)
+        interleave(on_scalar, h21, SECOND, odd)
         for u in range(OUT_TILES):
-            main_pass(2, 1, u, last=False)
-            main_pass(0, 1, u, last=True)
-            finish(1, u, by_scalar=(u % 2 == 0))
+            finish(EARLY, u, by_scalar=True)
+        interleave(on_vector, h11, FIRST, room)
+        quantise(h21, FIRST)
+        interleave(on_vector, h01, SECOND, room, at=4)
+        quantise(h11, FIRST)
+        quantise(h21, SECOND)
+        interleave(on_vector, h11, SECOND, room)
+        quantise(h01, SECOND)
+        quantise(h11, SECOND)
+        main_passes(0, MIDDLE)
+        main_passes(2, MIDDLE)
+        main_passes(1, MIDDLE, last=True)
+        for u in range(OUT_TILES):
+            finish(MIDDLE, u, by_scalar=True)
+        main_passes(2, LATE)
+        main_passes(0, LATE)
+        main_passes(1, LATE, last=True)
+        for u in range(OUT_TILES):
+            finish(LATE, u, by_scalar=(u < OUT_TILES // 2))

@@ -28,7 +28,7 @@ H_BLOCKS = H // K_PASS
 OUT_TILES = N // P
 QUADRANT = 32
 SCALE_ROWS = 4
-TABLE_HEAD = 3 * T // 8
+AHEAD = (8, 6, 2)
 BIAS_STEP = 4
 
 
@@ -56,7 +56,8 @@ def tile_list_paged_skip_adapter_kernel(
         w1_keys = [("w1", b, a) for b in range(H_BLOCKS) for a in range(K_PASSES)]
         w2_keys = [("w2", b) for b in range(H_BLOCKS)]
         h_keys = [("h", b, s) for b in range(H_BLOCKS) for s in range(HALVES)]
-        late_codes = [("h", 0, 0), ("h", 1, 0), ("h", 2, 0), ("h", 2, 1)]
+        h00, h10, h20, h01, h11, h21 = [("h", b, s) for s in range(HALVES) for b in range(H_BLOCKS)]
+        late_codes = [h00, h10, h20, h01, h21]
         planes, codes, scales = {}, {}, {}
         for key in w1_keys + w2_keys + h_keys:
             label = "".join(str(part) for part in key)
@@ -74,16 +75,15 @@ def tile_list_paged_skip_adapter_kernel(
 
         banks = [psum.tile([P, HALF], F32, name=f"bank{n}") for n in range(HALVES * OUT_TILES)]
 
-        nc.vector.memset(table_scales[:, : T // 8], 0)
-        nc.gpsimd.memset(table_scales[:, T // 8 :], 0)
         nc.vector.memset(bias_rows[:], 0.0)
+        nc.vector.memset(table_scales[QUADRANT : 2 * QUADRANT, :], 0)
+        nc.gpsimd.memset(table_scales[2 * QUADRANT :, :], 0)
         nc.vector.memset(v_scales[:].bitcast(I32), 0)
         nc.vector.memset(skip_scales[:].bitcast(I32), 0)
         make_identity(nc, identity[:])
 
-        def load_table(a, first, last):
-            words = tab_words[a].rearrange("p t i -> p (t i)").bitcast(I32)
-            nc.sync.dma_start(table[a][:, first:last], words[:, first:last])
+        def load_table(a):
+            nc.sync.dma_start(table[a][:], tab_words[a].rearrange("p t i -> p (t i)").bitcast(I32))
 
         def load_w1(b, a):
             rows = w1[a * K_PASS : (a + 1) * K_PASS, b * K_PASS : (b + 1) * K_PASS]
@@ -95,12 +95,11 @@ def tile_list_paged_skip_adapter_kernel(
 
         b2_row = BIAS_STEP * H_BLOCKS
         nc.sync.dma_start(offsets[:], offs)
-        load_table(0, 0, TABLE_HEAD)
         for a in range(K_PASSES):
             nc.sync.dma_start(table_scales[a:QUADRANT:K_PASSES, :], tab_scales[a].bitcast(I32))
+        load_table(0)
         nc.sync.dma_start(bias_rows[0:b2_row:BIAS_STEP, :], b1.rearrange("(b c) -> b c", b=H_BLOCKS))
         nc.sync.dma_start(bias_rows[b2_row : b2_row + 1, :], b2.rearrange("(o c) -> o c", o=1))
-        load_table(0, TABLE_HEAD, T)
         load_w1(0, 0)
         nc.vector.tensor_copy(picked_scales[:], table_scales[:].bitcast(U8).indirect(offsets[:]))
         picked_rows = K_PASSES * SCALE_ROWS
@@ -110,7 +109,7 @@ def tile_list_paged_skip_adapter_kernel(
                 picked_scales[picked_rows * q : picked_rows * (q + 1), :].bitcast(I32),
             )
         load_w1(0, 1)
-        load_table(1, 0, T)
+        load_table(1)
         for a in range(K_PASSES):
             load_w1(1, a)
 
@@ -128,14 +127,14 @@ def tile_list_paged_skip_adapter_kernel(
         def interleave(copy, key, share, tile, at=None):
             first, last = share
             at = first if at is None else at
-            room = tile[:, at * K_PASS : (at + last - first) * K_PASS]
+            place = tile[:, at * K_PASS : (at + last - first) * K_PASS]
             for n in range(first, last):
                 staged[key, n] = (tile, at + n - first)
             if key[0] == "w1":
-                dst = room.rearrange("p (t m h j) -> p m j h t", t=last - first, h=2, j=PACK)
+                dst = place.rearrange("p (t m h j) -> p m j h t", t=last - first, h=2, j=PACK)
                 src = planes[key][:].rearrange("p j (m h t) -> p m j h t", h=2, t=PACK)[:, :, :, :, first:last]
             else:
-                dst = room.rearrange("p (m i j) -> p m j i", i=PACK, j=PACK)
+                dst = place.rearrange("p (m i j) -> p m j i", i=PACK, j=PACK)
                 src = planes[key][:, :, first * P : last * P].rearrange("p j (m i) -> p m j i", i=PACK)
             copy(out=dst, in_=src)
 
@@ -161,7 +160,7 @@ def tile_list_paged_skip_adapter_kernel(
         def hidden_bank(b, s, t):
             return banks[t if s == 0 and b + 1 < H_BLOCKS else OUT_TILES + t]
 
-        def hidden_pass(b, s, t, a):
+        def hidden_pass(b, s, t, a, order):
             cols = slice(s * HALF, (s + 1) * HALF)
             key, bank = ("w1", b, a), hidden_bank(b, s, t)
             nc.tensor.matmul_mx(
@@ -170,24 +169,27 @@ def tile_list_paged_skip_adapter_kernel(
                 lhsT_scale=scales[key][:, t * P : (t + 1) * P],
                 rhs=v_words[a][:, cols].bitcast(FP8X4),
                 rhs_scale=v_scales[:, a, cols],
-                start=(a == 0),
-                stop=(a == K_PASSES - 1),
+                start=(a == order[0]),
+                stop=(a == order[-1]),
             )
-            if a == K_PASSES - 1:
+            if a == order[-1]:
                 nc.scalar.activation(planes[("h", b, s)][:, t, :], bank[:], ACT.Relu, bias=b1_cols[:, t, b : b + 1])
 
-        def hidden(b, halves):
+        def hidden(b, ahead):
+            tiles = [(s, t) for s in range(HALVES) for t in range(PACK)]
             for a in range(K_PASSES):
-                for s in halves:
-                    for t in range(PACK):
-                        hidden_pass(b, s, t, a)
+                for s, t in tiles[:ahead]:
+                    hidden_pass(b, s, t, a, range(K_PASSES))
+            for s, t in tiles[ahead:]:
+                for a in range(K_PASSES)[::-1]:
+                    hidden_pass(b, s, t, a, range(K_PASSES)[::-1])
 
         EARLY, MIDDLE, LATE = (0, HALF), (HALF, QUARTER), (HALF + QUARTER, QUARTER)
 
         def y_tile(group, u):
             first, width = group
-            place = (first * OUT_TILES + u * width)
-            return banks[place // HALF][:, place % HALF : place % HALF + width]
+            column = first * OUT_TILES + u * width
+            return banks[column // HALF][:, column % HALF : column % HALF + width]
 
         def skip_passes(group):
             first, width = group
@@ -231,8 +233,8 @@ def tile_list_paged_skip_adapter_kernel(
 
         gather_words(0, 0, S)
         for a, tile in enumerate((even, odd)):
-            interleave(on_vector, ("w1", 0, a), (0, 3), tile)
-            interleave(on_scalar, ("w1", 0, a), (3, 4), tile)
+            interleave(on_vector, ("w1", 0, a), (0, PACK - 1), tile)
+            interleave(on_scalar, ("w1", 0, a), (PACK - 1, PACK), tile)
             quantise(("w1", 0, a), WHOLE)
         for s in range(HALVES):
             gather_words(1, s * HALF, (s + 1) * HALF)
@@ -246,20 +248,14 @@ def tile_list_paged_skip_adapter_kernel(
         for b in range(H_BLOCKS):
             load_w2(b)
 
-        h00, h10, h20, h01, h11, h21 = [("h", b, s) for s in range(HALVES) for b in range(H_BLOCKS)]
-
-        hidden(0, range(HALVES))
+        hidden(0, AHEAD[0])
         prepare_in_two(("w1", 1, 0), even)
-        room = on_bytes_of("planes_w110", "staged_h00", PACK * HALF, BF16)
-        interleave(on_vector, h00, FIRST, room)
-        interleave(on_scalar, h00, SECOND, room)
         prepare_in_two(("w1", 1, 1), odd)
+        room = on_bytes_of("planes_w111", "staged_h00", PACK * HALF, BF16)
+        interleave(on_vector, h00, WHOLE, room)
 
-        hidden(1, range(HALVES))
-        room = on_bytes_of("planes_w111", "staged_h01", PACK * QUARTER, BF16)
-        interleave(on_vector, h01, FIRST, room)
+        hidden(1, AHEAD[1])
         interleave(on_vector, ("w1", 2, 0), FIRST, even)
-        quantise(h01, FIRST)
         interleave(on_vector, ("w1", 2, 0), SECOND, even)
         quantise(("w1", 2, 0), FIRST)
         codes[h00] = on_bytes_of("planes_w120", "codes_h00", HALF, U32)
@@ -271,10 +267,7 @@ def tile_list_paged_skip_adapter_kernel(
         interleave(on_scalar, h10, SECOND, room)
         skip_passes(EARLY)
 
-        hidden(2, [0])
-        for t in range(PACK):
-            for a in range(K_PASSES):
-                hidden_pass(2, 1, t, a)
+        hidden(2, AHEAD[2])
         interleave(on_vector, ("w2", 0), FIRST, even)
         interleave(on_vector, ("w2", 0), SECOND, even)
         quantise(("w2", 0), FIRST)
@@ -300,27 +293,30 @@ def tile_list_paged_skip_adapter_kernel(
         main_passes(2, EARLY, last=True)
         skip_passes(LATE)
 
-        room = on_bytes_of("staging0", "staged_late", 3 * PACK * QUARTER, BF16)
-        codes[h21] = on_bytes_of("planes_w21", "codes_h21", HALF, U32)
+        late = on_bytes_of("planes_w21", "codes_late", 2 * HALF, U32)
+        codes[h21], codes[h01] = late[:, :HALF], late[:, HALF:]
         interleave(on_scalar, h21, FIRST, odd)
         interleave(on_scalar, h21, SECOND, odd)
         for u in range(OUT_TILES):
             finish(EARLY, u, by_scalar=True)
+        room = on_bytes_of("staging0", "staged_late", 2 * PACK * HALF, BF16)
         interleave(on_vector, h11, FIRST, room)
         quantise(h21, FIRST)
-        interleave(on_vector, h01, SECOND, room, at=4)
+        interleave(on_vector, h01, FIRST, room, at=PACK + FIRST[0])
         quantise(h11, FIRST)
-        quantise(h21, SECOND)
         interleave(on_vector, h11, SECOND, room)
-        quantise(h01, SECOND)
+        quantise(h01, FIRST)
+        quantise(h21, SECOND)
+        interleave(on_vector, h01, SECOND, room, at=PACK + SECOND[0])
         quantise(h11, SECOND)
-        main_passes(0, MIDDLE)
+        quantise(h01, SECOND)
         main_passes(2, MIDDLE)
-        main_passes(1, MIDDLE, last=True)
+        main_passes(1, MIDDLE)
+        main_passes(0, MIDDLE, last=True)
         for u in range(OUT_TILES):
             finish(MIDDLE, u, by_scalar=True)
         main_passes(2, LATE)
-        main_passes(0, LATE)
-        main_passes(1, LATE, last=True)
+        main_passes(1, LATE)
+        main_passes(0, LATE, last=True)
         for u in range(OUT_TILES):
             finish(LATE, u, by_scalar=(u < OUT_TILES // 2))

@@ -93,13 +93,11 @@ def tile_list_paged_skip_adapter_kernel(
             rows = w2[b * K_PASS : (b + 1) * K_PASS, :]
             nc.sync.dma_start(planes[("w2", b)][:], rows.rearrange("(p j) c -> p j c", j=PACK))
 
-        b2_row = BIAS_STEP * H_BLOCKS
+        b1_end = BIAS_STEP * H_BLOCKS
         nc.sync.dma_start(offsets[:], offs)
-        for a in range(K_PASSES):
-            nc.sync.dma_start(table_scales[a:QUADRANT:K_PASSES, :], tab_scales[a].bitcast(I32))
+        nc.sync.dma_start(table_scales[:QUADRANT, :], tab_scales.rearrange("a q c -> q a c").bitcast(I32))
         load_table(0)
-        nc.sync.dma_start(bias_rows[0:b2_row:BIAS_STEP, :], b1.rearrange("(b c) -> b c", b=H_BLOCKS))
-        nc.sync.dma_start(bias_rows[b2_row : b2_row + 1, :], b2.rearrange("(o c) -> o c", o=1))
+        nc.sync.dma_start(bias_rows[0:b1_end:BIAS_STEP, :], b1.rearrange("(b c) -> b c", b=H_BLOCKS))
         load_w1(0, 0)
         nc.vector.tensor_copy(picked_scales[:], table_scales[:].bitcast(U8).indirect(offsets[:]))
         picked_rows = K_PASSES * SCALE_ROWS
@@ -114,11 +112,8 @@ def tile_list_paged_skip_adapter_kernel(
             load_w1(1, a)
 
         for t in range(PACK):
-            nc.tensor.transpose(banks[-2][:, t * P : (t + 1) * P], bias_rows[:, t::PACK], identity[:])
-        for u in range(OUT_TILES):
-            nc.tensor.transpose(banks[-1][:, u * P : (u + 1) * P], bias_rows[:, u * P : (u + 1) * P], identity[:])
-        nc.scalar.copy(out=b1_cols[:], in_=banks[-2][:].rearrange("p (t r) -> p t r", t=PACK)[:, :, 0:b2_row:BIAS_STEP])
-        nc.scalar.copy(out=b2_cols[:], in_=banks[-1][:].rearrange("p (u r) -> p u r", u=OUT_TILES)[:, :, b2_row])
+            nc.tensor.transpose(banks[-1][:, t * P : (t + 1) * P], bias_rows[:, t::PACK], identity[:])
+        nc.scalar.copy(out=b1_cols[:], in_=banks[-1][:].rearrange("p (t r) -> p t r", t=PACK)[:, :, 0:b1_end:BIAS_STEP])
 
         staged = {}
         on_vector, on_scalar = nc.vector.tensor_copy, nc.scalar.copy
@@ -193,20 +188,18 @@ def tile_list_paged_skip_adapter_kernel(
 
         def skip_passes(group):
             first, width = group
-            step = width if width == HALF else P
+            cols = slice(first, first + width)
             for u in range(OUT_TILES):
                 for a in range(K_PASSES):
-                    for c in range(0, width, step):
-                        cols = slice(first + c, first + c + step)
-                        nc.tensor.matmul_mx(
-                            y_tile(group, u)[:, c : c + step],
-                            lhsT=skip_words[:, a, 2 * u * P : 2 * (u + 1) * P].bitcast(FP4X4),
-                            lhsT_scale=skip_scales[:, a, u * P : (u + 1) * P],
-                            rhs=v_words[a][:, cols].bitcast(FP8X4),
-                            rhs_scale=v_scales[:, a, cols],
-                            start=(a == 0 and c == 0 and u * width % HALF == 0),
-                            stop=False,
-                        )
+                    nc.tensor.matmul_mx(
+                        y_tile(group, u),
+                        lhsT=skip_words[:, a, 2 * u * P : 2 * (u + 1) * P].bitcast(FP4X4),
+                        lhsT_scale=skip_scales[:, a, u * P : (u + 1) * P],
+                        rhs=v_words[a][:, cols].bitcast(FP8X4),
+                        rhs_scale=v_scales[:, a, cols],
+                        start=(a == 0 and u * width % HALF == 0),
+                        stop=False,
+                    )
 
         def main_passes(b, group, last=False):
             first, width = group
@@ -247,6 +240,8 @@ def tile_list_paged_skip_adapter_kernel(
             load_w1(2, a)
         for b in range(H_BLOCKS):
             load_w2(b)
+        with nc.allow_non_contiguous_dma(reason="one bias value a partition"):
+            nc.sync.dma_start(b2_cols[:], b2.rearrange("(u p) -> p u", p=P))
 
         hidden(0, AHEAD[0])
         prepare_in_two(("w1", 1, 0), even)

@@ -29,6 +29,8 @@ OUT_TILES = N // P
 QUADRANT = 32
 SCALE_ROWS = 4
 AHEAD = (8, 6, 2)
+SPAN = 256
+MOVING_WORDS, MOVING_SCALES, FIXED_WORDS, FIXED_SCALES = 0, 64, 128, 192
 BIAS_STEP = 4
 
 
@@ -40,14 +42,19 @@ def tile_list_paged_skip_adapter_kernel(
         keep = ctx.enter_context(tc.tile_pool(name="keep", bufs=1))
         psum = ctx.enter_context(tc.psum_pool(name="psum", bufs=1))
 
+        def shifted(name, rows, width, dtype, start, tag=None):
+            skip = start // (4 if dtype == U32 else 1)
+            tile = keep.tile([P, skip + rows * width], dtype, name=name, tag=tag or name, align_bytes=SPAN)
+            return tile[:, skip:] if rows == 1 else tile[:, skip:].rearrange("p (a c) -> p a c", a=rows)
+
         offsets = keep.tile([P, S // 16], U16, name="offsets")
-        table = [keep.tile([P, T], I32, name=f"table{a}", align_bytes=64) for a in range(K_PASSES)]
-        table_scales = keep.tile([P, T // 4], I32, name="table_scales", align_bytes=64)
-        picked_scales = keep.tile([P, S], U8, name="picked_scales", align_bytes=64)
-        v_words = [keep.tile([P, S], U32, name=f"v_words{a}", align_bytes=64) for a in range(K_PASSES)]
-        v_scales = keep.tile([P, K_PASSES, S], U8, name="v_scales", align_bytes=64)
-        skip_words = keep.tile([P, K_PASSES, 2 * N], U8, name="skip_words", align_bytes=64)
-        skip_scales = keep.tile([P, K_PASSES, N], U8, name="skip_scales", align_bytes=64)
+        table = [keep.tile([P, T], I32, name=f"table{a}", align_bytes=SPAN) for a in range(K_PASSES)]
+        table_scales = keep.tile([P, T // 4], I32, name="table_scales", align_bytes=SPAN)
+        picked_scales = keep.tile([P, S], U8, name="picked_scales", align_bytes=SPAN)
+        v_words = [keep.tile([P, S], U32, name=f"v_words{a}", align_bytes=SPAN) for a in range(K_PASSES)]
+        v_scales = shifted("v_scales", K_PASSES, S, U8, MOVING_SCALES)
+        skip_words = shifted("skip_words", K_PASSES, 2 * N, U8, FIXED_WORDS)
+        skip_scales = shifted("skip_scales", K_PASSES, N, U8, FIXED_SCALES)
         bias_rows = keep.tile([P, K_PASS], F32, name="bias_rows")
         identity = keep.tile([P, P], F32, name="identity")
         b1_cols = keep.tile([P, PACK, H_BLOCKS], F32, name="b1_cols")
@@ -62,16 +69,17 @@ def tile_list_paged_skip_adapter_kernel(
         for key in w1_keys + w2_keys + h_keys:
             label = "".join(str(part) for part in key)
             dtype = BF16 if key[0] == "h" else F32
-            planes[key] = keep.tile([P, PACK, K_PASS], dtype, name="planes_" + label, align_bytes=64)
+            planes[key] = keep.tile([P, PACK, K_PASS], dtype, name="planes_" + label, align_bytes=SPAN)
             if key not in late_codes:
-                codes[key] = keep.tile([P, K_PASS], U32, name="codes_" + label, align_bytes=64)
-            scales[key] = keep.tile([P, K_PASS], U8, name="scales_" + label, align_bytes=64)
+                start = MOVING_WORDS if key[0] == "h" else FIXED_WORDS
+                codes[key] = shifted("codes_" + label, 1, K_PASS, U32, start)
+            scales[key] = shifted("scales_" + label, 1, K_PASS, U8, MOVING_SCALES if key[0] == "h" else FIXED_SCALES)
 
-        staging = [keep.tile([P, K_PASS * PACK], BF16, name=f"staging{n}", align_bytes=64) for n in range(2)]
+        staging = [keep.tile([P, K_PASS * PACK], BF16, name=f"staging{n}", align_bytes=SPAN) for n in range(2)]
         even, odd = staging
 
         def on_bytes_of(tag, name, width, dtype):
-            return keep.tile([P, width], dtype, name=name, tag=tag, align_bytes=64)
+            return keep.tile([P, width], dtype, name=name, tag=tag, align_bytes=SPAN)
 
         banks = [psum.tile([P, HALF], F32, name=f"bank{n}") for n in range(HALVES * OUT_TILES)]
 

@@ -30,7 +30,7 @@ QUADRANT = 32
 SCALE_ROWS = 4
 AHEAD = (8, 6, 2)
 SPAN = 256
-MOVING_WORDS, MOVING_SCALES, FIXED_WORDS, FIXED_SCALES = 0, 64, 128, 192
+MOVING_WORDS, MOVING_SCALES, FIXED_WORDS, FIXED_SCALES = 0, 128, 192, 64
 BIAS_STEP = 4
 
 

from contextlib import ExitStack

import concourse.mybir as mybir
from concourse.masks import make_identity

K, H, N, T, S = 1024, 1536, 512, 2048, 1024
FLOPS = 2 * S * (K * H + H * N + K * N)

F32 = mybir.dt.float32
BF16 = mybir.dt.bfloat16
I32 = mybir.dt.int32
U32 = mybir.dt.uint32
U16 = mybir.dt.uint16
U8 = mybir.dt.uint8
FP8X4 = mybir.dt.float8_e4m3fn_x4
FP4X4 = mybir.dt.float4_e2m1fn_x4
ACT = mybir.ActivationFunctionType
ALU = mybir.AluOpType

P = 128
PACK = 4
K_PASS = P * PACK
HALF = 512
QUARTER = HALF // 2
HALVES = S // HALF
K_PASSES = K // K_PASS
H_BLOCKS = H // K_PASS
OUT_TILES = N // P
QUADRANT = 32
SCALE_ROWS = 4
AHEAD = (8, 6, 2)
SPAN = 256
MOVING_WORDS, MOVING_SCALES, FIXED_WORDS, FIXED_SCALES = 0, 128, 192, 64
BIAS_STEP = 4


def tile_list_paged_skip_adapter_kernel(
    tc, tab_words, tab_scales, offs, w1, b1, w2, ws_words, ws_scales, b2, out
):
    nc = tc.nc
    with ExitStack() as ctx:
        keep = ctx.enter_context(tc.tile_pool(name="keep", bufs=1))
        psum = ctx.enter_context(tc.psum_pool(name="psum", bufs=1))

        def shifted(name, rows, width, dtype, start, tag=None):
            skip = start // (4 if dtype == U32 else 1)
            tile = keep.tile([P, skip + rows * width], dtype, name=name, tag=tag or name, align_bytes=SPAN)
            return tile[:, skip:] if rows == 1 else tile[:, skip:].rearrange("p (a c) -> p a c", a=rows)

        offsets = keep.tile([P, S // 16], U16, name="offsets")
        table = [keep.tile([P, T], I32, name=f"table{a}", align_bytes=SPAN) for a in range(K_PASSES)]
        table_scales = keep.tile([P, T // 4], I32, name="table_scales", align_bytes=SPAN)
        picked_scales = keep.tile([P, S], U8, name="picked_scales", align_bytes=SPAN)
        v_words = [keep.tile([P, S], U32, name=f"v_words{a}", align_bytes=SPAN) for a in range(K_PASSES)]
        v_scales = shifted("v_scales", K_PASSES, S, U8, MOVING_SCALES)
        skip_words = shifted("skip_words", K_PASSES, 2 * N, U8, FIXED_WORDS)
        skip_scales = shifted("skip_scales", K_PASSES, N, U8, FIXED_SCALES)
        bias_rows = keep.tile([P, K_PASS], F32, name="bias_rows")
        identity = keep.tile([P, P], F32, name="identity")
        b1_cols = keep.tile([P, PACK, H_BLOCKS], F32, name="b1_cols")
        b2_cols = keep.tile([P, OUT_TILES], F32, name="b2_cols")

        w1_keys = [("w1", b, a) for b in range(H_BLOCKS) for a in range(K_PASSES)]
        w2_keys = [("w2", b) for b in range(H_BLOCKS)]
        h_keys = [("h", b, s) for b in range(H_BLOCKS) for s in range(HALVES)]
        h00, h10, h20, h01, h11, h21 = [("h", b, s) for s in range(HALVES) for b in range(H_BLOCKS)]
        late_codes = [h00, h10, h20, h01, h21]
        planes, codes, scales = {}, {}, {}
        for key in w1_keys + w2_keys + h_keys:
            label = "".join(str(part) for part in key)
            dtype = BF16 if key[0] == "h" else F32
            planes[key] = keep.tile([P, PACK, K_PASS], dtype, name="planes_" + label, align_bytes=SPAN)
            if key not in late_codes:
                start = MOVING_WORDS if key[0] == "h" else FIXED_WORDS
                codes[key] = shifted("codes_" + label, 1, K_PASS, U32, start)
            scales[key] = shifted("scales_" + label, 1, K_PASS, U8, MOVING_SCALES if key[0] == "h" else FIXED_SCALES)

        staging = [keep.tile([P, K_PASS * PACK], BF16, name=f"staging{n}", align_bytes=SPAN) for n in range(2)]
        even, odd = staging

        def on_bytes_of(tag, name, width, dtype):
            return keep.tile([P, width], dtype, name=name, tag=tag, align_bytes=SPAN)

        banks = [psum.tile([P, HALF], F32, name=f"bank{n}") for n in range(HALVES * OUT_TILES)]

        nc.vector.memset(bias_rows[:], 0.0)
        nc.vector.memset(table_scales[QUADRANT : 2 * QUADRANT, :], 0)
        nc.gpsimd.memset(table_scales[2 * QUADRANT :, :], 0)
        nc.vector.memset(v_scales[:].bitcast(I32), 0)
        nc.vector.memset(skip_scales[:].bitcast(I32), 0)
        make_identity(nc, identity[:])

        def load_table(a):
            nc.sync.dma_start(table[a][:], tab_words[a].rearrange("p t i -> p (t i)").bitcast(I32))

        def load_w1(b, a):
            rows = w1[a * K_PASS : (a + 1) * K_PASS, b * K_PASS : (b + 1) * K_PASS]
            nc.sync.dma_start(planes[("w1", b, a)][:], rows.rearrange("(p j) c -> p j c", j=PACK))

        def load_w2(b):
            rows = w2[b * K_PASS : (b + 1) * K_PASS, :]
            nc.sync.dma_start(planes[("w2", b)][:], rows.rearrange("(p j) c -> p j c", j=PACK))

        b1_end = BIAS_STEP * H_BLOCKS
        nc.sync.dma_start(offsets[:], offs)
        nc.sync.dma_start(table_scales[:QUADRANT, :], tab_scales.rearrange("a q c -> q a c").bitcast(I32))
        load_table(0)
        nc.sync.dma_start(bias_rows[0:b1_end:BIAS_STEP, :], b1.rearrange("(b c) -> b c", b=H_BLOCKS))
        load_w1(0, 0)
        nc.vector.tensor_copy(picked_scales[:], table_scales[:].bitcast(U8).indirect(offsets[:]))
        picked_rows = K_PASSES * SCALE_ROWS
        for q in (0, 2, 1, 3):
            nc.sync.dma_start(
                v_scales[QUADRANT * q : QUADRANT * q + SCALE_ROWS].bitcast(I32),
                picked_scales[picked_rows * q : picked_rows * (q + 1), :].bitcast(I32),
            )
        load_w1(0, 1)
        load_table(1)
        for a in range(K_PASSES):
            load_w1(1, a)

        for t in range(PACK):
            nc.tensor.transpose(banks[-1][:, t * P : (t + 1) * P], bias_rows[:, t::PACK], identity[:])
        nc.scalar.copy(out=b1_cols[:], in_=banks[-1][:].rearrange("p (t r) -> p t r", t=PACK)[:, :, 0:b1_end:BIAS_STEP])

        staged = {}
        on_vector, on_scalar = nc.vector.tensor_copy, nc.scalar.copy
        FIRST, SECOND, WHOLE = (0, 2), (2, 4), (0, 4)

        def interleave(copy, key, share, tile, at=None):
            first, last = share
            at = first if at is None else at
            place = tile[:, at * K_PASS : (at + last - first) * K_PASS]
            for n in range(first, last):
                staged[key, n] = (tile, at + n - first)
            if key[0] == "w1":
                dst = place.rearrange("p (t m h j) -> p m j h t", t=last - first, h=2, j=PACK)
                src = planes[key][:].rearrange("p j (m h t) -> p m j h t", h=2, t=PACK)[:, :, :, :, first:last]
            else:
                dst = place.rearrange("p (m i j) -> p m j i", i=PACK, j=PACK)
                src = planes[key][:, :, first * P : last * P].rearrange("p j (m i) -> p m j i", i=PACK)
            copy(out=dst, in_=src)

        def quantise(key, share):
            first, last = share
            tile, at = staged[key, first]
            nc.vector.quantize_mx(
                out=codes[key][:, first * P : last * P].bitcast(FP8X4),
                scales=scales[key][:, first * P : last * P],
                in_=tile[:, at * K_PASS : (at + last - first) * K_PASS],
            )

        def prepare_in_two(key, tile):
            for share in (FIRST, SECOND):
                interleave(on_vector, key, share, tile)
            for share in (FIRST, SECOND):
                quantise(key, share)

        def gather_words(a, first, last):
            picks = offsets[:, first // 16 : last // 16]
            nc.vector.tensor_copy(v_words[a][:, first:last], table[a][:].bitcast(U32).indirect(picks))

        def hidden_bank(b, s, t):
            return banks[t if s == 0 and b + 1 < H_BLOCKS else OUT_TILES + t]

        def hidden_pass(b, s, t, a, order):
            cols = slice(s * HALF, (s + 1) * HALF)
            key, bank = ("w1", b, a), hidden_bank(b, s, t)
            nc.tensor.matmul_mx(
                bank[:],
                lhsT=codes[key][:, t * P : (t + 1) * P].bitcast(FP8X4),
                lhsT_scale=scales[key][:, t * P : (t + 1) * P],
                rhs=v_words[a][:, cols].bitcast(FP8X4),
                rhs_scale=v_scales[:, a, cols],
                start=(a == order[0]),
                stop=(a == order[-1]),
            )
            if a == order[-1]:
                nc.scalar.activation(planes[("h", b, s)][:, t, :], bank[:], ACT.Relu, bias=b1_cols[:, t, b : b + 1])

        def hidden(b, ahead):
            tiles = [(s, t) for s in range(HALVES) for t in range(PACK)]
            for a in range(K_PASSES):
                for s, t in tiles[:ahead]:
                    hidden_pass(b, s, t, a, range(K_PASSES))
            for s, t in tiles[ahead:]:
                for a in range(K_PASSES)[::-1]:
                    hidden_pass(b, s, t, a, range(K_PASSES)[::-1])

        EARLY, MIDDLE, LATE = (0, HALF), (HALF, QUARTER), (HALF + QUARTER, QUARTER)

        def y_tile(group, u):
            first, width = group
            column = first * OUT_TILES + u * width
            return banks[column // HALF][:, column % HALF : column % HALF + width]

        def skip_passes(group):
            first, width = group
            cols = slice(first, first + width)
            for u in range(OUT_TILES):
                for a in range(K_PASSES):
                    nc.tensor.matmul_mx(
                        y_tile(group, u),
                        lhsT=skip_words[:, a, 2 * u * P : 2 * (u + 1) * P].bitcast(FP4X4),
                        lhsT_scale=skip_scales[:, a, u * P : (u + 1) * P],
                        rhs=v_words[a][:, cols].bitcast(FP8X4),
                        rhs_scale=v_scales[:, a, cols],
                        start=(a == 0 and u * width % HALF == 0),
                        stop=False,
                    )

        def main_passes(b, group, last=False):
            first, width = group
            key, cols = ("h", b, first // HALF), slice(first % HALF, first % HALF + width)
            for u in range(OUT_TILES):
                nc.tensor.matmul_mx(
                    y_tile(group, u),
                    lhsT=codes[("w2", b)][:, u * P : (u + 1) * P].bitcast(FP8X4),
                    lhsT_scale=scales[("w2", b)][:, u * P : (u + 1) * P],
                    rhs=codes[key][:, cols].bitcast(FP8X4),
                    rhs_scale=scales[key][:, cols],
                    start=False,
                    stop=(last and (u + 1) * width % HALF == 0),
                )

        def finish(group, u, by_scalar):
            first, width = group
            result = keep.tile([P, width], F32, name=f"result{first}_{u}")
            if by_scalar:
                nc.scalar.activation(result[:], y_tile(group, u), ACT.Identity, bias=b2_cols[:, u : u + 1])
            else:
                nc.vector.tensor_scalar(result[:], y_tile(group, u), b2_cols[:, u : u + 1], None, op0=ALU.add)
            nc.sync.dma_start(out[u * P : (u + 1) * P, first : first + width], result[:])

        gather_words(0, 0, S)
        for a, tile in enumerate((even, odd)):
            interleave(on_vector, ("w1", 0, a), (0, PACK - 1), tile)
            interleave(on_scalar, ("w1", 0, a), (PACK - 1, PACK), tile)
            quantise(("w1", 0, a), WHOLE)
        for s in range(HALVES):
            gather_words(1, s * HALF, (s + 1) * HALF)

        for r in range(SCALE_ROWS):
            rows = ws_scales[:, r::SCALE_ROWS, :].rearrange("a q c -> q a c")
            nc.sync.dma_start(skip_scales[:].bitcast(I32)[r:P:QUADRANT, :, :], rows.bitcast(I32))
        nc.sync.dma_start(skip_words[:].bitcast(I32), ws_words.rearrange("a p c -> p a c").bitcast(I32))
        for a in range(K_PASSES):
            load_w1(2, a)
        for b in range(H_BLOCKS):
            load_w2(b)
        with nc.allow_non_contiguous_dma(reason="one bias value a partition"):
            nc.sync.dma_start(b2_cols[:], b2.rearrange("(u p) -> p u", p=P))

        hidden(0, AHEAD[0])
        prepare_in_two(("w1", 1, 0), even)
        prepare_in_two(("w1", 1, 1), odd)
        room = on_bytes_of("planes_w111", "staged_h00", PACK * HALF, BF16)
        interleave(on_vector, h00, WHOLE, room)

        hidden(1, AHEAD[1])
        interleave(on_vector, ("w1", 2, 0), FIRST, even)
        interleave(on_vector, ("w1", 2, 0), SECOND, even)
        quantise(("w1", 2, 0), FIRST)
        codes[h00] = on_bytes_of("planes_w120", "codes_h00", HALF, U32)
        quantise(h00, WHOLE)
        quantise(("w1", 2, 0), SECOND)
        prepare_in_two(("w1", 2, 1), odd)
        room = on_bytes_of("planes_w121", "staged_h10", PACK * HALF, BF16)
        interleave(on_vector, h10, FIRST, room)
        interleave(on_scalar, h10, SECOND, room)
        skip_passes(EARLY)

        hidden(2, AHEAD[2])
        interleave(on_vector, ("w2", 0), FIRST, even)
        interleave(on_vector, ("w2", 0), SECOND, even)
        quantise(("w2", 0), FIRST)
        codes[h10] = on_bytes_of("planes_w20", "codes_h10", HALF, U32)
        quantise(h10, WHOLE)
        quantise(("w2", 0), SECOND)
        interleave(on_vector, ("w2", 1), FIRST, odd)
        interleave(on_vector, ("w2", 1), SECOND, odd)
        quantise(("w2", 1), FIRST)
        room = on_bytes_of("planes_w21", "staged_h20", PACK * HALF, BF16)
        interleave(on_vector, h20, FIRST, room)
        interleave(on_scalar, h20, SECOND, room)
        quantise(("w2", 1), SECOND)
        interleave(on_vector, ("w2", 2), FIRST, even)
        interleave(on_vector, ("w2", 2), SECOND, even)
        quantise(("w2", 2), FIRST)
        codes[h20] = on_bytes_of("planes_w22", "codes_h20", HALF, U32)
        quantise(h20, WHOLE)
        quantise(("w2", 2), SECOND)
        main_passes(0, EARLY)
        main_passes(1, EARLY)
        skip_passes(MIDDLE)
        main_passes(2, EARLY, last=True)
        skip_passes(LATE)

        late = on_bytes_of("planes_w21", "codes_late", 2 * HALF, U32)
        codes[h21], codes[h01] = late[:, :HALF], late[:, HALF:]
        interleave(on_scalar, h21, FIRST, odd)
        interleave(on_scalar, h21, SECOND, odd)
        for u in range(OUT_TILES):
            finish(EARLY, u, by_scalar=True)
        room = on_bytes_of("staging0", "staged_late", 2 * PACK * HALF, BF16)
        interleave(on_vector, h11, FIRST, room)
        quantise(h21, FIRST)
        interleave(on_vector, h01, FIRST, room, at=PACK + FIRST[0])
        quantise(h11, FIRST)
        interleave(on_vector, h11, SECOND, room)
        quantise(h01, FIRST)
        quantise(h21, SECOND)
        interleave(on_vector, h01, SECOND, room, at=PACK + SECOND[0])
        quantise(h11, SECOND)
        quantise(h01, SECOND)
        main_passes(2, MIDDLE)
        main_passes(1, MIDDLE)
        main_passes(0, MIDDLE, last=True)
        for u in range(OUT_TILES):
            finish(MIDDLE, u, by_scalar=True)
        main_passes(2, LATE)
        main_passes(1, LATE)
        main_passes(0, LATE, last=True)
        for u in range(OUT_TILES):
            finish(LATE, u, by_scalar=(u < OUT_TILES // 2))
